import numpy as np
import ml_dtypes


def mxq(x, axis, fmt="e4m3"):
    dtype, down = {"e4m3": (ml_dtypes.float8_e4m3fn, 7), "e5m2": (ml_dtypes.float8_e5m2, 14)}[fmt]
    v = np.moveaxis(np.asarray(x, np.float32).astype(ml_dtypes.bfloat16).astype(np.float64), axis, -1)
    blocks = v.reshape(v.shape[:-1] + (-1, 32))
    amax = np.abs(blocks).max(-1, keepdims=True)
    byte = np.maximum(np.where(amax > 0, np.frexp(amax)[1] - 1 + 127, 0) - down, 1)
    scale = np.exp2(byte - 127.0)
    codes = (blocks / scale).astype(np.float32).astype(dtype).astype(np.float64)
    return np.moveaxis((codes * scale).reshape(v.shape), -1, axis)


WIDE = False


def mx_kscale(k):
    if not WIDE:
        return np.ones(k)
    levels = np.array([10, -10, 5, -5, 0])
    if k % 512:
        return np.exp2(np.random.permutation(np.resize(levels, k // 32))).repeat(32)
    a = np.empty((k // 512, 16))
    for p in range(k // 512):
        a[p, :8] = np.random.permutation(np.resize(levels, 8))
        for g in range(8):
            far = levels[np.abs(levels - a[p, g]) >= 10]
            a[p, g + 8] = far[np.random.randint(len(far))]
    return np.exp2(a.ravel()).repeat(32)


def f64(x):
    return np.asarray(x).astype(np.float64)


def striped(idx):
    return np.tile(idx.reshape(-1, 16).T, (8, 1)).astype(np.uint16)


def unstriped(offs):
    return offs[:16].T.reshape(-1).astype(np.int64)


def relu(v):
    return np.maximum(v, 0.0)


K, T, E, C, H, N = 2048, 512, 6, 256, 512, 128
TOP = 3


def by_expert(wq, xq):
    return np.concatenate([wq[e].T @ xq[:, e * C:(e + 1) * C] for e in range(E)], axis=1)


def setup_inputs():
    n = np.random.standard_normal
    s = mx_kscale(K)[:, None]
    u = mx_kscale(H)
    deal = np.repeat(np.arange(E), C).reshape(TOP, T)[:, np.random.permutation(T)]
    deal = np.take_along_axis(deal, np.argsort(np.random.rand(TOP, T), axis=0), axis=0)
    for _ in range(8):
        s_, t_ = np.random.permutation(T).reshape(2, -1); r = np.random.randint(TOP, size=T // 2); x, y = deal[r, s_].copy(), deal[r, t_].copy()
        ok = ~((deal[:, s_] == y).any(0) | (deal[:, t_] == x).any(0)); deal[r[ok], s_[ok]] = y[ok]; deal[r[ok], t_[ok]] = x[ok]
    order = np.lexsort((np.random.rand(TOP * T), deal.reshape(-1)))
    slot_token = order % T; pos = np.empty(TOP * T, np.int64); pos[order] = np.arange(TOP * T); pos = pos.reshape(TOP, T)
    g = np.random.uniform(0.5, 1.5, (TOP, T)); g = g / g.sum(0)
    return {
        "xT": (n((K, T)) * s).astype(np.float32),
        "w1": (n((E, K, H)) / np.sqrt(K) / s[None] * u[None, None, :]).astype(np.float32),
        "w2": (n((E, H, N)) / np.sqrt(H) / u[None, :, None]).astype(np.float32),
        "gate": np.stack([np.tile(r, (N, 1)) for r in g]).astype(np.float32),
        "offs": striped(slot_token),
        "pos1": striped(pos[0]),
        "pos2": striped(pos[1]),
        "pos3": striped(pos[2]),
    }


def reference(xT, w1, w2, gate, offs, pos1, pos2, pos3):
    idx = unstriped(offs)
    xq = mxq(f64(xT)[:, idx], 0, "e4m3")
    h = relu(by_expert(mxq(f64(w1), 1, "e4m3"), xq))
    y = by_expert(mxq(f64(w2), 1, "e4m3"), mxq(h, 0, "e4m3"))
    return sum(f64(gate[r]) * y[:, unstriped(p)] for r, p in enumerate((pos1, pos2, pos3)))

@@ -1,0 +1,211 @@
+from contextlib import ExitStack
+
+import concourse.mybir as mybir
+
+K, T, E, C, H, N, TOP = 2048, 512, 6, 256, 512, 128, 3
+
+FLOPS = 2 * TOP * T * (K * H + H * N)
+
+F32 = mybir.dt.float32
+BF16 = mybir.dt.bfloat16
+U32 = mybir.dt.uint32
+U16 = mybir.dt.uint16
+U8 = mybir.dt.uint8
+FP8X4 = mybir.dt.float8_e4m3fn_x4
+COPY = mybir.ActivationFunctionType.Copy
+RELU = mybir.ActivationFunctionType.Relu
+ADD = mybir.AluOpType.add
+MULT = mybir.AluOpType.mult
+
+P = 128
+J = 4
+S = K // (P * J)
+HT = H // P
+M = H // HT
+LIST = C // 16
+VECTOR_SHARE = (0, 16, 64, 0)
+LAST_SHARE = (64, 32, 48, 88)
+REPEATS = (0, 0, 0, 0)
+
+
+def tile_moe_tk_mlp_relu_kernel(tc, xT, w1, w2, gate, offs, pos1, pos2, pos3, out):
+    nc = tc.nc
+    with ExitStack() as ctx:
+        keep = ctx.enter_context(tc.tile_pool(name="keep", bufs=1))
+        stage = ctx.enter_context(tc.tile_pool(name="stage", bufs=12))
+        groups = ctx.enter_context(tc.tile_pool(name="groups", bufs=4))
+        work = ctx.enter_context(tc.tile_pool(name="work", bufs=3))
+        codes = ctx.enter_context(tc.tile_pool(name="codes", bufs=8))
+        psum = ctx.enter_context(tc.psum_pool(name="psum", bufs=8))
+
+        def load(rows):
+            raw = stage.tile([P, J, rows.shape[1]], F32, name="raw", tag="raw", align_bytes=64)
+            nc.sync.dma_start(out=raw[:], in_=rows.rearrange("(p j) c -> p j c", j=J))
+            return raw[:]
+
+        x_scales = keep.tile([P, T], U8, name="x_scales", align_bytes=64)
+        nc.gpsimd.memset(x_scales[:], 0)
+        offsets = keep.tile([P, TOP * T // 16], U16, name="offsets")
+        x_words = []
+        for s in range(S):
+            if s == S // 2:
+                nc.sync.dma_start(offsets[:], offs)
+            raw = load(xT[s * P * J : (s + 1) * P * J, :])
+            grouped = groups.tile([P, T, J], BF16, name="xg", tag="grouped", align_bytes=64)
+            nc.scalar.activation(
+                grouped[:].rearrange("p (c i) j -> p c j i", i=4), raw.rearrange("p j (c i) -> p c j i", i=4), COPY
+            )
+            words = keep.tile([P, T], U32, name=f"x_words{s}", align_bytes=64)
+            nc.vector.quantize_mx(
+                out=words[:].bitcast(FP8X4),
+                scales=x_scales[4 * s :, :],
+                in_=grouped[:].rearrange("p t j -> p (t j)"),
+            )
+            x_words.append(words)
+
+        w2_words = keep.tile([P, E, N], U32, name="w2_words", align_bytes=64)
+        w2_scales = keep.tile([P, E, N], U8, name="w2_scales", align_bytes=64)
+        y = keep.tile([P, E * C], F32, name="y", align_bytes=64)
+
+        def gather(e):
+            words = work.tile([P, S, C], U32, name="slot_words", align_bytes=64)
+            scales = work.tile([P, C], U8, name="slot_scales", align_bytes=64)
+            where = offsets[:, e * LIST : (e + 1) * LIST]
+            for s in range(S):
+                nc.vector.tensor_copy(words[:, s, :], x_words[s][:].indirect(where))
+            nc.vector.tensor_copy(scales[:], x_scales[:].indirect(where))
+            return words, scales
+
+        def chunk(raw, cut, step):
+            grouped = groups.tile([P, H, J], BF16, name="wg", tag="grouped", align_bytes=64)
+            src = raw.rearrange("p j (m t) -> p m j t", t=HT)
+            dst = grouped[:].rearrange("p (t m) j -> p m j t", t=HT)
+            if cut > 0:
+                nc.vector.tensor_copy(out=dst[:, :cut], in_=src[:, :cut])
+            if cut < M:
+                nc.scalar.activation(dst[:, cut:], src[:, cut:], COPY)
+            words = codes.tile([P, H], U32, name="w1_words", align_bytes=64)
+            scales = codes.tile([P, H], U8, name="w1_scales", align_bytes=64)
+            for lo in range(0, H, step):
+                nc.vector.quantize_mx(
+                    out=words[:, lo : lo + step].bitcast(FP8X4),
+                    scales=scales[:, lo : lo + step],
+                    in_=grouped[:, lo : lo + step, :].rearrange("p h j -> p (h j)"),
+                )
+            return words, scales
+
+        def second_weights(e0, e1, on_vector):
+            raw = stage.tile([P, e1 - e0, J * N], F32, name="raw", tag="raw", align_bytes=64)
+            nc.sync.dma_start(out=raw[:], in_=w2[e0:e1].rearrange("e (p j) n -> p e (j n)", j=J))
+            grouped = groups.tile([P, e1 - e0, N, J], BF16, name="w2g", tag="grouped", align_bytes=64)
+            src = raw[:].rearrange("p e (j n) -> p e n j", j=J)
+            if on_vector:
+                nc.vector.tensor_copy(out=grouped[:], in_=src)
+            else:
+                nc.scalar.activation(grouped[:], src, COPY)
+            nc.vector.quantize_mx(
+                out=w2_words[:, e0:e1, :].rearrange("p e n -> p (e n)").bitcast(FP8X4),
+                scales=w2_scales[:, e0:e1, :].rearrange("p e n -> p (e n)"),
+                in_=grouped[:].rearrange("p e n j -> p (e n j)"),
+            )
+
+        def second(e, lo, hi, copy_out):
+            acc = psum.tile([P, C], F32, name="y_acc", tag="bank")
+            words, scales = hidden[e]
+            nc.tensor.matmul_mx(
+                out=acc[:, : hi - lo],
+                lhsT=w2_words[:, e, :].bitcast(FP8X4),
+                lhsT_scale=w2_scales[:, e, :],
+                rhs=words[:, lo:hi].bitcast(FP8X4),
+                rhs_scale=scales[:, lo:hi],
+                start=True,
+                stop=True,
+            )
+            copy_out(y[:, e * C + lo : e * C + hi], acc[:, : hi - lo])
+
+        hidden = []
+        slots = gather(0)
+        for e in range(E):
+            last = e == E - 1
+            banks = []
+            for t in range(HT):
+                bank = psum.tile([P, C], F32, name="h_acc", tag="bank")
+                banks.append(bank)
+            for s in range(S):
+                words, scales = chunk(
+                    load(w1[e, s * P * J : (s + 1) * P * J, :]), (LAST_SHARE if last else VECTOR_SHARE)[s], M if last and s == S - 1 else H
+                )
+                if s == S - 1 and not last:
+                    next_slots = gather(e + 1)
+
+                def product(acc, t, start, stop):
+                    nc.tensor.matmul_mx(
+                        out=acc,
+                        lhsT=words[:, t * M : (t + 1) * M].bitcast(FP8X4),
+                        lhsT_scale=scales[:, t * M : (t + 1) * M],
+                        rhs=slots[0][:, s, :].bitcast(FP8X4),
+                        rhs_scale=slots[1][4 * s :, :],
+                        start=start,
+                        stop=stop,
+                    )
+
+                for t in range(HT):
+                    product(banks[t][:], t, s == 0, s == S - 1)
+                if last and REPEATS[s] > 0:
+                    spare = psum.tile([P, C], F32, name="spare", tag="bank")
+                    for r in range(REPEATS[s]):
+                        product(spare[:], r % HT, True, True)
+            if last:
+                second_weights(0, 2, True)
+                second_weights(2, 4, False)
+                second_weights(4, 6, True)
+                for d in range(E - 1):
+                    second(d, 0, C, nc.scalar.copy)
+                places = []
+                for r, pos in enumerate((pos1, pos2, pos3)):
+                    place = keep.tile([P, T // 16], U16, name=f"place{r}")
+                    nc.sync.dma_start(place[:], pos)
+                    places.append(place)
+                gates = stage.tile([P, TOP, T], F32, name="raw", tag="raw", align_bytes=64)
+                for r in range(TOP):
+                    nc.sync.dma_start(out=gates[:, r, :], in_=gate[r])
+            h_rows = work.tile([P, HT, C], BF16, name="h_rows", align_bytes=64)
+            for t in range(HT):
+                if last and t % 2 == 0:
+                    nc.scalar.activation(h_rows[:, t, :], banks[t][:], RELU)
+                else:
+                    nc.vector.tensor_scalar_max(h_rows[:, t, :], banks[t][:], 0.0)
+            h_grouped = work.tile([P, C, HT], BF16, name="h_grouped", align_bytes=64)
+            h_words = codes.tile([P, C], U32, name="h_words", align_bytes=64)
+            h_scales = codes.tile([P, C], U8, name="h_scales", align_bytes=64)
+            hidden.append((h_words, h_scales))
+            parts = [(0, C // 2), (C // 2, C)] if last else [(0, C)]
+            for lo, hi in parts:
+                nc.vector.tensor_copy(
+                    out=h_grouped[:, lo:hi, :].rearrange("p (c i) t -> p c t i", i=4),
+                    in_=h_rows[:, :, lo:hi].rearrange("p t (c i) -> p c t i", i=4),
+                )
+            for lo, hi in parts:
+                nc.vector.quantize_mx(
+                    out=h_words[:, lo:hi].bitcast(FP8X4),
+                    scales=h_scales[:, lo:hi],
+                    in_=h_grouped[:, lo:hi, :].rearrange("p c t -> p (c t)"),
+                )
+            if last:
+                for lo, hi in parts:
+                    second(e, lo, hi, nc.vector.tensor_copy)
+            slots = next_slots
+
+        products = []
+        for r in range(TOP):
+            scaled = keep.tile([P, T], F32, name=f"scaled{r}", align_bytes=64)
+            nc.vector.tensor_tensor(scaled[:], y[:].indirect(places[r][:]), gates[:, r, :], MULT)
+            products.append(scaled)
+        pair = keep.tile([P, T], F32, name="pair", align_bytes=64)
+        total = keep.tile([P, T], F32, name="total", align_bytes=64)
+        halves = [slice(0, T // 2), slice(T // 2, T)]
+        for cols in halves:
+            nc.vector.tensor_tensor(pair[:, cols], products[0][:, cols], products[1][:, cols], ADD)
+        for cols in halves:
+            nc.vector.tensor_tensor(total[:, cols], pair[:, cols], products[2][:, cols], ADD)
+            nc.sync.dma_start(out=out[:, cols], in_=total[:, cols])

@@ -23,18 +23,30 @@ S = K // (P * J)
 HT = H // P
 M = H // HT
 LIST = C // 16
-VECTOR_SHARE = (0, 16, 64, 0)
-LAST_SHARE = (64, 32, 48, 88)
-REPEATS = (0, 0, 0, 0)
+HALF = C // 2
+X_SHARE = (16, 16, 16, 16)
+SHARE = ((44,) * 4, (44,) * 4, (44,) * 4, (44,) * 4, (68,) * 4, (68, 68, 68, 84))
+HOLD = (2, 2, 2, 2, 2, 1)
+SLOTS = 3
+GROUPS = 6
+W2_EARLY = ()
+W2_LATE = ((0, 1, "s"), (1, 2, "s"), (2, 3, "v"), (3, 4, "s"), (4, 5, "s"), (5, 6, "v"))
+RELU_V = (1, 3)
+YCOPY = "sssssv"
+LAST_FUSED = False
+COMB = 0
+EARLY_AT = 18
+GHOLD = {3: (5, 6), 4: (9, 10), 5: (13, 14)}
+STAGE = 11
 
 
 def tile_moe_tk_mlp_relu_kernel(tc, xT, w1, w2, gate, offs, pos1, pos2, pos3, out):
     nc = tc.nc
     with ExitStack() as ctx:
         keep = ctx.enter_context(tc.tile_pool(name="keep", bufs=1))
-        stage = ctx.enter_context(tc.tile_pool(name="stage", bufs=12))
-        groups = ctx.enter_context(tc.tile_pool(name="groups", bufs=4))
-        work = ctx.enter_context(tc.tile_pool(name="work", bufs=3))
+        stage = ctx.enter_context(tc.tile_pool(name="stage", bufs=STAGE))
+        groups = ctx.enter_context(tc.tile_pool(name="groups", bufs=GROUPS))
+        work = ctx.enter_context(tc.tile_pool(name="work", bufs=SLOTS))
         codes = ctx.enter_context(tc.tile_pool(name="codes", bufs=8))
         psum = ctx.enter_context(tc.psum_pool(name="psum", bufs=8))
 
@@ -42,6 +54,12 @@ def tile_moe_tk_mlp_relu_kernel(tc, xT, w1, w2, gate, offs, pos1, pos2, pos3, ou
             raw = stage.tile([P, J, rows.shape[1]], F32, name="raw", tag="raw", align_bytes=64)
             nc.sync.dma_start(out=raw[:], in_=rows.rearrange("(p j) c -> p j c", j=J))
             return raw[:]
+
+        def shared_copy(dst, src, cut):
+            if cut > 0:
+                nc.vector.tensor_copy(out=dst[:, :cut], in_=src[:, :cut])
+            if cut < dst.shape[1]:
+                nc.scalar.activation(dst[:, cut:], src[:, cut:], COPY)
 
         x_scales = keep.tile([P, T], U8, name="x_scales", align_bytes=64)
         nc.gpsimd.memset(x_scales[:], 0)
@@ -52,8 +70,8 @@ def tile_moe_tk_mlp_relu_kernel(tc, xT, w1, w2, gate, offs, pos1, pos2, pos3, ou
                 nc.sync.dma_start(offsets[:], offs)
             raw = load(xT[s * P * J : (s + 1) * P * J, :])
             grouped = groups.tile([P, T, J], BF16, name="xg", tag="grouped", align_bytes=64)
-            nc.scalar.activation(
-                grouped[:].rearrange("p (c i) j -> p c j i", i=4), raw.rearrange("p j (c i) -> p c j i", i=4), COPY
+            shared_copy(
+                grouped[:].rearrange("p (c i) j -> p c j i", i=4), raw.rearrange("p j (c i) -> p c j i", i=4), X_SHARE[s]
             )
             words = keep.tile([P, T], U32, name=f"x_words{s}", align_bytes=64)
             nc.vector.quantize_mx(
@@ -63,27 +81,30 @@ def tile_moe_tk_mlp_relu_kernel(tc, xT, w1, w2, gate, offs, pos1, pos2, pos3, ou
             )
             x_words.append(words)
 
-        w2_words = keep.tile([P, E, N], U32, name="w2_words", align_bytes=64)
-        w2_scales = keep.tile([P, E, N], U8, name="w2_scales", align_bytes=64)
         y = keep.tile([P, E * C], F32, name="y", align_bytes=64)
 
         def gather(e):
-            words = work.tile([P, S, C], U32, name="slot_words", align_bytes=64)
-            scales = work.tile([P, C], U8, name="slot_scales", align_bytes=64)
+            words = keep.tile([P, S, C], U32, name="slot_words", tag=f"words{e}", align_bytes=64)
+            scales = keep.tile([P, C], U8, name="slot_scales", tag=f"scales{e}", align_bytes=64)
             where = offsets[:, e * LIST : (e + 1) * LIST]
             for s in range(S):
                 nc.vector.tensor_copy(words[:, s, :], x_words[s][:].indirect(where))
             nc.vector.tensor_copy(scales[:], x_scales[:].indirect(where))
             return words, scales
 
-        def chunk(raw, cut, step):
-            grouped = groups.tile([P, H, J], BF16, name="wg", tag="grouped", align_bytes=64)
-            src = raw.rearrange("p j (m t) -> p m j t", t=HT)
-            dst = grouped[:].rearrange("p (t m) j -> p m j t", t=HT)
-            if cut > 0:
-                nc.vector.tensor_copy(out=dst[:, :cut], in_=src[:, :cut])
-            if cut < M:
-                nc.scalar.activation(dst[:, cut:], src[:, cut:], COPY)
+        lent = {}
+        for e in GHOLD:
+            lent[GHOLD[e][0]] = f"words{e}"
+            lent[GHOLD[e][1]] = f"scales{e}"
+
+        def chunk(raw, k, cut, step):
+            if k in lent:
+                grouped = keep.tile([P, H, J], BF16, name="wg", tag=lent[k], align_bytes=64)
+            else:
+                grouped = groups.tile([P, H, J], BF16, name="wg", tag="grouped", align_bytes=64)
+            shared_copy(
+                grouped[:].rearrange("p (t m) j -> p m j t", t=HT), raw.rearrange("p j (m t) -> p m j t", t=HT), cut
+            )
             words = codes.tile([P, H], U32, name="w1_words", align_bytes=64)
             scales = codes.tile([P, H], U8, name="w1_scales", align_bytes=64)
             for lo in range(0, H, step):
@@ -94,112 +115,164 @@ def tile_moe_tk_mlp_relu_kernel(tc, xT, w1, w2, gate, offs, pos1, pos2, pos3, ou
                 )
             return words, scales
 
-        def second_weights(e0, e1, on_vector):
+        second_w = {}
+
+        def second_load(e0, e1):
             raw = stage.tile([P, e1 - e0, J * N], F32, name="raw", tag="raw", align_bytes=64)
             nc.sync.dma_start(out=raw[:], in_=w2[e0:e1].rearrange("e (p j) n -> p e (j n)", j=J))
+            return raw
+
+        def second_weights(raw, e0, e1, eng):
             grouped = groups.tile([P, e1 - e0, N, J], BF16, name="w2g", tag="grouped", align_bytes=64)
-            src = raw[:].rearrange("p e (j n) -> p e n j", j=J)
-            if on_vector:
-                nc.vector.tensor_copy(out=grouped[:], in_=src)
-            else:
-                nc.scalar.activation(grouped[:], src, COPY)
+            for e in range(e1 - e0):
+                shared_copy(
+                    grouped[:, e].rearrange("p (c i) j -> p c j i", i=4),
+                    raw[:, e, :].rearrange("p (j c i) -> p c j i", j=J, i=4),
+                    32 if eng[e] == "v" else 0,
+                )
+            words = keep.tile([P, e1 - e0, N], U32, name=f"w2_words{e0}", align_bytes=64)
+            scales = keep.tile([P, e1 - e0, N], U8, name=f"w2_scales{e0}", align_bytes=64)
             nc.vector.quantize_mx(
-                out=w2_words[:, e0:e1, :].rearrange("p e n -> p (e n)").bitcast(FP8X4),
-                scales=w2_scales[:, e0:e1, :].rearrange("p e n -> p (e n)"),
+                out=words[:].rearrange("p e n -> p (e n)").bitcast(FP8X4),
+                scales=scales[:].rearrange("p e n -> p (e n)"),
                 in_=grouped[:].rearrange("p e n j -> p (e n j)"),
             )
+            for e in range(e0, e1):
+                second_w[e] = (words[:, e - e0, :], scales[:, e - e0, :])
 
-        def second(e, lo, hi, copy_out):
+        def second(e, lo, hi, eng):
             acc = psum.tile([P, C], F32, name="y_acc", tag="bank")
             words, scales = hidden[e]
             nc.tensor.matmul_mx(
                 out=acc[:, : hi - lo],
-                lhsT=w2_words[:, e, :].bitcast(FP8X4),
-                lhsT_scale=w2_scales[:, e, :],
+                lhsT=second_w[e][0].bitcast(FP8X4),
+                lhsT_scale=second_w[e][1],
                 rhs=words[:, lo:hi].bitcast(FP8X4),
                 rhs_scale=scales[:, lo:hi],
                 start=True,
                 stop=True,
             )
+            copy_out = nc.vector.tensor_copy if eng == "v" else nc.scalar.copy
             copy_out(y[:, e * C + lo : e * C + hi], acc[:, : hi - lo])
 
-        hidden = []
-        slots = gather(0)
-        for e in range(E):
-            last = e == E - 1
-            banks = []
-            for t in range(HT):
-                bank = psum.tile([P, C], F32, name="h_acc", tag="bank")
-                banks.append(bank)
-            for s in range(S):
-                words, scales = chunk(
-                    load(w1[e, s * P * J : (s + 1) * P * J, :]), (LAST_SHARE if last else VECTOR_SHARE)[s], M if last and s == S - 1 else H
-                )
-                if s == S - 1 and not last:
-                    next_slots = gather(e + 1)
+        def product(acc, weights, t, slots, s, lo, hi):
+            nc.tensor.matmul_mx(
+                out=acc,
+                lhsT=weights[0][:, t * M : (t + 1) * M].bitcast(FP8X4),
+                lhsT_scale=weights[1][:, t * M : (t + 1) * M],
+                rhs=slots[0][:, s, lo:hi].bitcast(FP8X4),
+                rhs_scale=slots[1][4 * s :, lo:hi],
+                start=s == 0,
+                stop=s == S - 1,
+            )
 
-                def product(acc, t, start, stop):
-                    nc.tensor.matmul_mx(
-                        out=acc,
-                        lhsT=words[:, t * M : (t + 1) * M].bitcast(FP8X4),
-                        lhsT_scale=scales[:, t * M : (t + 1) * M],
-                        rhs=slots[0][:, s, :].bitcast(FP8X4),
-                        rhs_scale=slots[1][4 * s :, :],
-                        start=start,
-                        stop=stop,
-                    )
-
-                for t in range(HT):
-                    product(banks[t][:], t, s == 0, s == S - 1)
-                if last and REPEATS[s] > 0:
-                    spare = psum.tile([P, C], F32, name="spare", tag="bank")
-                    for r in range(REPEATS[s]):
-                        product(spare[:], r % HT, True, True)
-            if last:
-                second_weights(0, 2, True)
-                second_weights(2, 4, False)
-                second_weights(4, 6, True)
-                for d in range(E - 1):
-                    second(d, 0, C, nc.scalar.copy)
-                places = []
-                for r, pos in enumerate((pos1, pos2, pos3)):
-                    place = keep.tile([P, T // 16], U16, name=f"place{r}")
-                    nc.sync.dma_start(place[:], pos)
-                    places.append(place)
-                gates = stage.tile([P, TOP, T], F32, name="raw", tag="raw", align_bytes=64)
-                for r in range(TOP):
-                    nc.sync.dma_start(out=gates[:, r, :], in_=gate[r])
-            h_rows = work.tile([P, HT, C], BF16, name="h_rows", align_bytes=64)
-            for t in range(HT):
-                if last and t % 2 == 0:
-                    nc.scalar.activation(h_rows[:, t, :], banks[t][:], RELU)
-                else:
-                    nc.vector.tensor_scalar_max(h_rows[:, t, :], banks[t][:], 0.0)
-            h_grouped = work.tile([P, C, HT], BF16, name="h_grouped", align_bytes=64)
-            h_words = codes.tile([P, C], U32, name="h_words", align_bytes=64)
-            h_scales = codes.tile([P, C], U8, name="h_scales", align_bytes=64)
-            hidden.append((h_words, h_scales))
-            parts = [(0, C // 2), (C // 2, C)] if last else [(0, C)]
-            for lo, hi in parts:
-                nc.vector.tensor_copy(
-                    out=h_grouped[:, lo:hi, :].rearrange("p (c i) t -> p c t i", i=4),
-                    in_=h_rows[:, :, lo:hi].rearrange("p t (c i) -> p c t i", i=4),
-                )
+        def quantise_hidden(e, h_grouped, parts):
+            h_words = keep.tile([P, C], U32, name=f"h_words{e}", align_bytes=64)
+            h_scales = keep.tile([P, C], U8, name=f"h_scales{e}", align_bytes=64)
+            hidden[e] = (h_words, h_scales)
             for lo, hi in parts:
                 nc.vector.quantize_mx(
                     out=h_words[:, lo:hi].bitcast(FP8X4),
                     scales=h_scales[:, lo:hi],
                     in_=h_grouped[:, lo:hi, :].rearrange("p c t -> p (c t)"),
                 )
-            if last:
-                for lo, hi in parts:
-                    second(e, lo, hi, nc.vector.tensor_copy)
-            slots = next_slots
+
+        def first_layer(weights, slots):
+            banks = []
+            for lo, hi in parts:
+                bank = psum.tile([P, HT, HALF], F32, name="h_acc", tag="bank")
+                for t in range(HT):
+                    for s in range(S):
+                        product(bank[:, t, :], weights[s], t, slots, s, lo, hi)
+                banks.append(bank)
+            return banks
+
+        def hidden_out(e, banks, raw):
+            h_grouped = raw[:, 0, :].bitcast(BF16).rearrange("p (c t) -> p c t", t=HT)
+            for (lo, hi), bank in zip(parts, banks):
+                nc.scalar.activation(h_grouped[:, lo:hi, :], bank[:].rearrange("p t c -> p c t"), RELU)
+            quantise_hidden(e, h_grouped, [(0, C)])
+
+        hidden = {}
+        parts = [(0, HALF), (HALF, C)]
+        slots = {e: gather(e) for e in range(E) if e not in GHOLD}
+        banks = None
+        for e in range(E):
+            last = e == E - 1
+            weights = []
+            if last and not LAST_FUSED:
+                tiles = [psum.tile([P, C], F32, name="h_acc", tag="bank") for t in range(HT)]
+            for s in range(S):
+                raw = load(w1[e, s * P * J : (s + 1) * P * J, :])
+                weights.append(chunk(raw, e * S + s, SHARE[e][s], M if last and s == S - 1 else H))
+                if last and not LAST_FUSED:
+                    for t in range(HT):
+                        product(tiles[t][:], weights[s], t, slots[e], s, 0, C)
+                if s == HOLD[e] and e > 0:
+                    hidden_out(e - 1, banks, raw)
+                for d in GHOLD:
+                    if max(GHOLD[d]) == e * S + s:
+                        slots[d] = gather(d)
+                if e * S + s == EARLY_AT:
+                    for e0, e1, eng in W2_EARLY:
+                        second_weights(second_load(e0, e1), e0, e1, eng)
+                if e * S + s > EARLY_AT and last and s == HOLD[e]:
+                    for e0, e1, eng in W2_EARLY:
+                        for d in range(e0, min(e1, E - 1)):
+                            second(d, 0, C, YCOPY[d])
+            if not last:
+                banks = first_layer(weights, slots[e])
+
+        e = E - 1
+        raws = [second_load(e0, e1) for e0, e1, eng in W2_LATE]
+        h_grouped = keep.tile([P, C, HT], BF16, name="h_grouped", align_bytes=64)
+        if LAST_FUSED:
+            fb = [psum.tile([P, HT, HALF], F32, name="h_acc", tag="bank") for h in range(2)]
+            for t in range(HT):
+                for (lo, hi), bank in zip(parts, fb):
+                    for s in range(S):
+                        product(bank[:, t, :], weights[s], t, slots[e], s, lo, hi)
+            nc.scalar.activation(h_grouped[:, :HALF, :], fb[0][:].rearrange("p t c -> p c t"), RELU)
+            nc.vector.tensor_scalar_max(h_grouped[:, HALF:, :], fb[1][:].rearrange("p t c -> p c t"), 0.0)
+        else:
+            h_rows = keep.tile([P, HT, C], BF16, name="h_rows", align_bytes=64)
+            for t in range(HT):
+                if t in RELU_V:
+                    nc.vector.tensor_scalar_max(h_rows[:, t, :], tiles[t][:], 0.0)
+                else:
+                    nc.scalar.activation(h_rows[:, t, :], tiles[t][:], RELU)
+            for lo, hi in parts:
+                nc.vector.tensor_copy(
+                    out=h_grouped[:, lo:hi, :].rearrange("p (c i) t -> p c t i", i=4),
+                    in_=h_rows[:, :, lo:hi].rearrange("p t (c i) -> p c t i", i=4),
+                )
+        quantise_hidden(e, h_grouped, parts)
+        if e in second_w:
+            for lo, hi in parts:
+                second(e, lo, hi, YCOPY[e])
+        for raw, (e0, e1, eng) in zip(raws, W2_LATE):
+            second_weights(raw, e0, e1, eng)
+            for d in range(e0, e1):
+                if d == e:
+                    for lo, hi in parts:
+                        second(e, lo, hi, YCOPY[e])
+                else:
+                    second(d, 0, C, YCOPY[d])
+        places = []
+        for r, pos in enumerate((pos1, pos2, pos3)):
+            place = keep.tile([P, T // 16], U16, name=f"place{r}")
+            nc.sync.dma_start(place[:], pos)
+            places.append(place)
+        gates = []
+        for r in range(TOP):
+            g = keep.tile([P, T], F32, name=f"gate{r}", align_bytes=64)
+            nc.sync.dma_start(out=g[:], in_=gate[r])
+            gates.append(g)
 
         products = []
         for r in range(TOP):
             scaled = keep.tile([P, T], F32, name=f"scaled{r}", align_bytes=64)
-            nc.vector.tensor_tensor(scaled[:], y[:].indirect(places[r][:]), gates[:, r, :], MULT)
+            nc.vector.tensor_tensor(scaled[:], y[:].indirect(places[r][:]), gates[r][:], MULT)
             products.append(scaled)
         pair = keep.tile([P, T], F32, name="pair", align_bytes=64)
         total = keep.tile([P, T], F32, name="total", align_bytes=64)

@@ -25,19 +25,27 @@ M = H // HT
 LIST = C // 16
 HALF = C // 2
 X_SHARE = (16, 16, 16, 16)
-SHARE = ((44,) * 4, (44,) * 4, (44,) * 4, (44,) * 4, (68,) * 4, (68, 68, 68, 84))
+SHARE = ((40,) * 4,) * 4 + ((84, 84, 64, 84), (84, 64, 84, 84))
 HOLD = (2, 2, 2, 2, 2, 1)
 SLOTS = 3
-GROUPS = 6
+GROUPS = 5
 W2_EARLY = ()
-W2_LATE = ((0, 1, "s"), (1, 2, "s"), (2, 3, "v"), (3, 4, "s"), (4, 5, "s"), (5, 6, "v"))
-RELU_V = (1, 3)
-YCOPY = "sssssv"
+W2_LATE = tuple((e, e + 1, "ssvvvv"[e]) for e in range(6))
+RELU_V = ()
+YCOPY = "sssssvs"
 LAST_FUSED = False
 COMB = 0
 EARLY_AT = 18
-GHOLD = {3: (5, 6), 4: (9, 10), 5: (13, 14)}
+GHOLD = {3: (5, 7), 4: (9, 11), 5: (13, 15)}
 STAGE = 11
+S_ONLY = True
+QHOLD = {}
+QSTEP = 128
+CUT = 256
+LAST_PIECES = ((128, 92),)
+W2_SPLIT = 2
+X_LOADS = (1, 1, 1, 1)
+LOADS = ((1, 1, 1, 1),) * 6
 
 
 def tile_moe_tk_mlp_relu_kernel(tc, xT, w1, w2, gate, offs, pos1, pos2, pos3, out):
@@ -50,10 +58,15 @@ def tile_moe_tk_mlp_relu_kernel(tc, xT, w1, w2, gate, offs, pos1, pos2, pos3, ou
         codes = ctx.enter_context(tc.tile_pool(name="codes", bufs=8))
         psum = ctx.enter_context(tc.psum_pool(name="psum", bufs=8))
 
-        def load(rows):
-            raw = stage.tile([P, J, rows.shape[1]], F32, name="raw", tag="raw", align_bytes=64)
-            nc.sync.dma_start(out=raw[:], in_=rows.rearrange("(p j) c -> p j c", j=J))
-            return raw[:]
+        def load(rows, s, sizes, got):
+            if s == len(got):
+                count = sizes[[sum(sizes[:i]) for i in range(len(sizes))].index(s)]
+                raw = stage.tile([P, count, J * H], F32, name="raw", tag="raw", align_bytes=64)
+                nc.sync.dma_start(
+                    out=raw[:], in_=rows[s * P * J : (s + count) * P * J, :].rearrange("(s p j) c -> p s (j c)", p=P, j=J)
+                )
+                got.extend(raw[:, i, :].rearrange("p (j c) -> p j c", j=J) for i in range(count))
+            return got[s]
 
         def shared_copy(dst, src, cut):
             if cut > 0:
@@ -65,10 +78,11 @@ def tile_moe_tk_mlp_relu_kernel(tc, xT, w1, w2, gate, offs, pos1, pos2, pos3, ou
         nc.gpsimd.memset(x_scales[:], 0)
         offsets = keep.tile([P, TOP * T // 16], U16, name="offsets")
         x_words = []
+        got = []
         for s in range(S):
             if s == S // 2:
                 nc.sync.dma_start(offsets[:], offs)
-            raw = load(xT[s * P * J : (s + 1) * P * J, :])
+            raw = load(xT, s, X_LOADS, got)
             grouped = groups.tile([P, T, J], BF16, name="xg", tag="grouped", align_bytes=64)
             shared_copy(
                 grouped[:].rearrange("p (c i) j -> p c j i", i=4), raw.rearrange("p j (c i) -> p c j i", i=4), X_SHARE[s]
@@ -92,7 +106,7 @@ def tile_moe_tk_mlp_relu_kernel(tc, xT, w1, w2, gate, offs, pos1, pos2, pos3, ou
             nc.vector.tensor_copy(scales[:], x_scales[:].indirect(where))
             return words, scales
 
-        lent = {}
+        lent = {QHOLD[e]: f"h_words{e}" for e in QHOLD}
         for e in GHOLD:
             lent[GHOLD[e][0]] = f"words{e}"
             lent[GHOLD[e][1]] = f"scales{e}"
@@ -102,9 +116,17 @@ def tile_moe_tk_mlp_relu_kernel(tc, xT, w1, w2, gate, offs, pos1, pos2, pos3, ou
                 grouped = keep.tile([P, H, J], BF16, name="wg", tag=lent[k], align_bytes=64)
             else:
                 grouped = groups.tile([P, H, J], BF16, name="wg", tag="grouped", align_bytes=64)
-            shared_copy(
-                grouped[:].rearrange("p (t m) j -> p m j t", t=HT), raw.rearrange("p j (m t) -> p m j t", t=HT), cut
-            )
+            dst = grouped[:].rearrange("p (t m) j -> p m j t", t=HT)
+            if raw is None:
+                m0 = 0
+                for width, share in LAST_PIECES:
+                    piece = stage.tile([P, J, width * HT], F32, name="raw", tag="raw", align_bytes=64)
+                    rows = w1[E - 1, (S - 1) * P * J :, m0 * HT : (m0 + width) * HT]
+                    nc.sync.dma_start(out=piece[:], in_=rows.rearrange("(p j) c -> p j c", j=J))
+                    shared_copy(dst[:, m0 : m0 + width], piece[:].rearrange("p j (m t) -> p m j t", t=HT), share)
+                    m0 = m0 + width
+            else:
+                shared_copy(dst, raw.rearrange("p j (m t) -> p m j t", t=HT), cut)
             words = codes.tile([P, H], U32, name="w1_words", align_bytes=64)
             scales = codes.tile([P, H], U8, name="w1_scales", align_bytes=64)
             for lo in range(0, H, step):
@@ -123,12 +145,18 @@ def tile_moe_tk_mlp_relu_kernel(tc, xT, w1, w2, gate, offs, pos1, pos2, pos3, ou
             return raw
 
         def second_weights(raw, e0, e1, eng):
+            if e1 - e0 > 1 and W2_SPLIT:
+                for e in range(e0, e1):
+                    second_weights(raw[:, e - e0 : e - e0 + 1, :], e, e + 1, eng[e - e0])
+                    if W2_SPLIT > 1:
+                        finish(e)
+                return
             grouped = groups.tile([P, e1 - e0, N, J], BF16, name="w2g", tag="grouped", align_bytes=64)
             for e in range(e1 - e0):
                 shared_copy(
                     grouped[:, e].rearrange("p (c i) j -> p c j i", i=4),
                     raw[:, e, :].rearrange("p (j c i) -> p c j i", j=J, i=4),
-                    32 if eng[e] == "v" else 0,
+                    eng[e] if isinstance(eng[e], int) else (32 if eng[e] == "v" else 0),
                 )
             words = keep.tile([P, e1 - e0, N], U32, name=f"w2_words{e0}", align_bytes=64)
             scales = keep.tile([P, e1 - e0, N], U8, name=f"w2_scales{e0}", align_bytes=64)
@@ -166,15 +194,16 @@ def tile_moe_tk_mlp_relu_kernel(tc, xT, w1, w2, gate, offs, pos1, pos2, pos3, ou
                 stop=s == S - 1,
             )
 
-        def quantise_hidden(e, h_grouped, parts):
-            h_words = keep.tile([P, C], U32, name=f"h_words{e}", align_bytes=64)
+        def quantise_hidden(e, pieces):
+            h_words = keep.tile([P, C], U32, name=f"h_words{e}", tag=f"h_words{e}", align_bytes=64)
             h_scales = keep.tile([P, C], U8, name=f"h_scales{e}", align_bytes=64)
             hidden[e] = (h_words, h_scales)
-            for lo, hi in parts:
+            width = C // len(pieces)
+            for i, piece in enumerate(pieces):
                 nc.vector.quantize_mx(
-                    out=h_words[:, lo:hi].bitcast(FP8X4),
-                    scales=h_scales[:, lo:hi],
-                    in_=h_grouped[:, lo:hi, :].rearrange("p c t -> p (c t)"),
+                    out=h_words[:, i * width : (i + 1) * width].bitcast(FP8X4),
+                    scales=h_scales[:, i * width : (i + 1) * width],
+                    in_=piece,
                 )
 
         def first_layer(weights, slots):
@@ -188,10 +217,22 @@ def tile_moe_tk_mlp_relu_kernel(tc, xT, w1, w2, gate, offs, pos1, pos2, pos3, ou
             return banks
 
         def hidden_out(e, banks, raw):
-            h_grouped = raw[:, 0, :].bitcast(BF16).rearrange("p (c t) -> p c t", t=HT)
-            for (lo, hi), bank in zip(parts, banks):
-                nc.scalar.activation(h_grouped[:, lo:hi, :], bank[:].rearrange("p t c -> p c t"), RELU)
-            quantise_hidden(e, h_grouped, [(0, C)])
+            if S_ONLY:
+                halves = [raw[:, i, H // 2 :].bitcast(BF16) for i in range(2)]
+            else:
+                halves = [raw[:, 0, i * H // 2 : (i + 1) * H // 2].bitcast(BF16) for i in range(2)]
+            for half, bank in zip(halves, banks):
+                nc.scalar.activation(
+                    half.rearrange("p (c t) -> p c t", t=HT), bank[:].rearrange("p t c -> p c t"), RELU
+                )
+            return halves if S_ONLY else [raw[:, 0, :].bitcast(BF16)]
+
+        def finish(d):
+            if d == E - 1:
+                for i, (lo, hi) in enumerate(parts):
+                    second(d, lo, hi, YCOPY[d + i])
+            else:
+                second(d, 0, C, YCOPY[d])
 
         hidden = {}
         parts = [(0, HALF), (HALF, C)]
@@ -200,23 +241,29 @@ def tile_moe_tk_mlp_relu_kernel(tc, xT, w1, w2, gate, offs, pos1, pos2, pos3, ou
         for e in range(E):
             last = e == E - 1
             weights = []
+            got = []
             if last and not LAST_FUSED:
                 tiles = [psum.tile([P, C], F32, name="h_acc", tag="bank") for t in range(HT)]
             for s in range(S):
-                raw = load(w1[e, s * P * J : (s + 1) * P * J, :])
-                weights.append(chunk(raw, e * S + s, SHARE[e][s], M if last and s == S - 1 else H))
+                raw = None if last and s == S - 1 else load(w1[e], s, LOADS[e], got)
+                weights.append(chunk(raw, e * S + s, SHARE[e][s], QSTEP if last and s == S - 1 else H))
                 if last and not LAST_FUSED:
                     for t in range(HT):
                         product(tiles[t][:], weights[s], t, slots[e], s, 0, C)
                 if s == HOLD[e] and e > 0:
-                    hidden_out(e - 1, banks, raw)
+                    waiting = hidden_out(e - 1, banks, raw)
+                    if e - 1 not in QHOLD:
+                        quantise_hidden(e - 1, waiting)
+                for d in QHOLD:
+                    if QHOLD[d] == e * S + s:
+                        quantise_hidden(d, waiting)
                 for d in GHOLD:
                     if max(GHOLD[d]) == e * S + s:
                         slots[d] = gather(d)
                 if e * S + s == EARLY_AT:
                     for e0, e1, eng in W2_EARLY:
                         second_weights(second_load(e0, e1), e0, e1, eng)
-                if e * S + s > EARLY_AT and last and s == HOLD[e]:
+                if e * S + s == EARLY_AT + 1:
                     for e0, e1, eng in W2_EARLY:
                         for d in range(e0, min(e1, E - 1)):
                             second(d, 0, C, YCOPY[d])
@@ -246,37 +293,33 @@ def tile_moe_tk_mlp_relu_kernel(tc, xT, w1, w2, gate, offs, pos1, pos2, pos3, ou
                     out=h_grouped[:, lo:hi, :].rearrange("p (c i) t -> p c t i", i=4),
                     in_=h_rows[:, :, lo:hi].rearrange("p t (c i) -> p c t i", i=4),
                 )
-        quantise_hidden(e, h_grouped, parts)
+        quantise_hidden(e, [h_grouped[:, lo:hi, :].rearrange("p c t -> p (c t)") for lo, hi in parts])
         if e in second_w:
             for lo, hi in parts:
                 second(e, lo, hi, YCOPY[e])
         for raw, (e0, e1, eng) in zip(raws, W2_LATE):
             second_weights(raw, e0, e1, eng)
-            for d in range(e0, e1):
-                if d == e:
-                    for lo, hi in parts:
-                        second(e, lo, hi, YCOPY[e])
-                else:
-                    second(d, 0, C, YCOPY[d])
+            if e1 - e0 == 1 or W2_SPLIT < 2:
+                for d in range(e0, e1):
+                    finish(d)
         places = []
         for r, pos in enumerate((pos1, pos2, pos3)):
             place = keep.tile([P, T // 16], U16, name=f"place{r}")
             nc.sync.dma_start(place[:], pos)
             places.append(place)
-        gates = []
+        gate_tile = stage.tile([P, TOP, T], F32, name="raw", tag="raw", align_bytes=64)
+        gates = [gate_tile[:, r, :] for r in range(TOP)]
         for r in range(TOP):
-            g = keep.tile([P, T], F32, name=f"gate{r}", align_bytes=64)
-            nc.sync.dma_start(out=g[:], in_=gate[r])
-            gates.append(g)
+            nc.sync.dma_start(out=gates[r], in_=gate[r])
 
         products = []
         for r in range(TOP):
             scaled = keep.tile([P, T], F32, name=f"scaled{r}", align_bytes=64)
-            nc.vector.tensor_tensor(scaled[:], y[:].indirect(places[r][:]), gates[r][:], MULT)
+            nc.vector.tensor_tensor(scaled[:], y[:].indirect(places[r][:]), gates[r], MULT)
             products.append(scaled)
         pair = keep.tile([P, T], F32, name="pair", align_bytes=64)
         total = keep.tile([P, T], F32, name="total", align_bytes=64)
-        halves = [slice(0, T // 2), slice(T // 2, T)]
+        halves = [slice(0, CUT), slice(CUT, T)]
         for cols in halves:
             nc.vector.tensor_tensor(pair[:, cols], products[0][:, cols], products[1][:, cols], ADD)
         for cols in halves:

@@ -30,19 +30,21 @@ HOLD = (2, 2, 2, 2, 2, 1)
 SLOTS = 3
 GROUPS = 5
 W2_EARLY = ()
-W2_LATE = tuple((e, e + 1, "ssvvvv"[e]) for e in range(6))
+W2_LATE = tuple((e, e + 1, "ssvvss"[e]) for e in range(6))
 RELU_V = ()
-YCOPY = "sssssvs"
+YCOPY = "ssssvvs"
 LAST_FUSED = False
 COMB = 0
 EARLY_AT = 18
 GHOLD = {3: (5, 7), 4: (9, 11), 5: (13, 15)}
 STAGE = 11
+H_AT = 6
+FINISH_LATE = True
 S_ONLY = True
 QHOLD = {}
 QSTEP = 128
 CUT = 256
-LAST_PIECES = ((128, 92),)
+LAST_PIECES = ((128, 84),)
 W2_SPLIT = 2
 X_LOADS = (1, 1, 1, 1)
 LOADS = ((1, 1, 1, 1),) * 6
@@ -273,35 +275,32 @@ def tile_moe_tk_mlp_relu_kernel(tc, xT, w1, w2, gate, offs, pos1, pos2, pos3, ou
         e = E - 1
         raws = [second_load(e0, e1) for e0, e1, eng in W2_LATE]
         h_grouped = keep.tile([P, C, HT], BF16, name="h_grouped", align_bytes=64)
-        if LAST_FUSED:
-            fb = [psum.tile([P, HT, HALF], F32, name="h_acc", tag="bank") for h in range(2)]
-            for t in range(HT):
-                for (lo, hi), bank in zip(parts, fb):
-                    for s in range(S):
-                        product(bank[:, t, :], weights[s], t, slots[e], s, lo, hi)
-            nc.scalar.activation(h_grouped[:, :HALF, :], fb[0][:].rearrange("p t c -> p c t"), RELU)
-            nc.vector.tensor_scalar_max(h_grouped[:, HALF:, :], fb[1][:].rearrange("p t c -> p c t"), 0.0)
-        else:
-            h_rows = keep.tile([P, HT, C], BF16, name="h_rows", align_bytes=64)
-            for t in range(HT):
-                if t in RELU_V:
-                    nc.vector.tensor_scalar_max(h_rows[:, t, :], tiles[t][:], 0.0)
-                else:
-                    nc.scalar.activation(h_rows[:, t, :], tiles[t][:], RELU)
+        h_rows = keep.tile([P, HT, C], BF16, name="h_rows", align_bytes=64)
+        for t in range(HT):
+            if t in RELU_V:
+                nc.vector.tensor_scalar_max(h_rows[:, t, :], tiles[t][:], 0.0)
+            else:
+                nc.scalar.activation(h_rows[:, t, :], tiles[t][:], RELU)
+
+        def last_hidden():
             for lo, hi in parts:
                 nc.vector.tensor_copy(
                     out=h_grouped[:, lo:hi, :].rearrange("p (c i) t -> p c t i", i=4),
                     in_=h_rows[:, :, lo:hi].rearrange("p t (c i) -> p c t i", i=4),
                 )
-        quantise_hidden(e, [h_grouped[:, lo:hi, :].rearrange("p c t -> p (c t)") for lo, hi in parts])
-        if e in second_w:
-            for lo, hi in parts:
-                second(e, lo, hi, YCOPY[e])
-        for raw, (e0, e1, eng) in zip(raws, W2_LATE):
+            quantise_hidden(e, [h_grouped[:, lo:hi, :].rearrange("p c t -> p (c t)") for lo, hi in parts])
+
+        for i, (raw, (e0, e1, eng)) in enumerate(zip(raws, W2_LATE)):
+            if i == H_AT:
+                last_hidden()
             second_weights(raw, e0, e1, eng)
-            if e1 - e0 == 1 or W2_SPLIT < 2:
-                for d in range(e0, e1):
-                    finish(d)
+            if not FINISH_LATE:
+                finish(e0)
+        if H_AT == len(raws):
+            last_hidden()
+        if FINISH_LATE:
+            for e0, e1, eng in W2_LATE:
+                finish(e0)
         places = []
         for r, pos in enumerate((pos1, pos2, pos3)):
             place = keep.tile([P, T // 16], U16, name=f"place{r}")

@@ -20,307 +20,210 @@ MULT = mybir.AluOpType.mult
 P = 128
 J = 4
 S = K // (P * J)
-HT = H // P
-M = H // HT
-LIST = C // 16
+M = P
+HT = H // M
 HALF = C // 2
-X_SHARE = (16, 16, 16, 16)
-SHARE = ((40,) * 4,) * 4 + ((84, 84, 64, 84), (84, 64, 84, 84))
-HOLD = (2, 2, 2, 2, 2, 1)
-SLOTS = 3
-GROUPS = 5
-W2_EARLY = ()
-W2_LATE = tuple((e, e + 1, "ssvvss"[e]) for e in range(6))
-RELU_V = ()
-YCOPY = "ssssvvs"
-LAST_FUSED = False
-COMB = 0
-EARLY_AT = 18
-GHOLD = {3: (5, 7), 4: (9, 11), 5: (13, 15)}
-STAGE = 11
-H_AT = 6
-FINISH_LATE = True
-S_ONLY = True
-QHOLD = {}
-QSTEP = 128
-CUT = 256
-LAST_PIECES = ((128, 84),)
-W2_SPLIT = 2
-X_LOADS = (1, 1, 1, 1)
-LOADS = ((1, 1, 1, 1),) * 6
+HALVES = ((0, HALF), (HALF, C))
+LIST = C // 16
+SCALE_ROWS = 4
+
+X_SHARE = 16
+SHARE_WHILE_GATHERING = 40
+SHARE_AFTER = 84
+EARLY_EXPERTS = 3
+GATHER_AHEAD = 2
+GATHER_WORDS_AT = 1
+GATHER_SCALES_AT = 3
+HIDDEN_AT = 2
+W2_ON_VECTOR = range(2, 4)
+
+STAGE_BUFS = 11
+GROUPED_BUFS = 5
+CODE_BUFS = 2 * S
 
 
 def tile_moe_tk_mlp_relu_kernel(tc, xT, w1, w2, gate, offs, pos1, pos2, pos3, out):
     nc = tc.nc
     with ExitStack() as ctx:
         keep = ctx.enter_context(tc.tile_pool(name="keep", bufs=1))
-        stage = ctx.enter_context(tc.tile_pool(name="stage", bufs=STAGE))
-        groups = ctx.enter_context(tc.tile_pool(name="groups", bufs=GROUPS))
-        work = ctx.enter_context(tc.tile_pool(name="work", bufs=SLOTS))
-        codes = ctx.enter_context(tc.tile_pool(name="codes", bufs=8))
+        stage = ctx.enter_context(tc.tile_pool(name="stage", bufs=STAGE_BUFS))
+        groups = ctx.enter_context(tc.tile_pool(name="groups", bufs=GROUPED_BUFS))
+        codes = ctx.enter_context(tc.tile_pool(name="codes", bufs=CODE_BUFS))
         psum = ctx.enter_context(tc.psum_pool(name="psum", bufs=8))
 
-        def load(rows, s, sizes, got):
-            if s == len(got):
-                count = sizes[[sum(sizes[:i]) for i in range(len(sizes))].index(s)]
-                raw = stage.tile([P, count, J * H], F32, name="raw", tag="raw", align_bytes=64)
-                nc.sync.dma_start(
-                    out=raw[:], in_=rows[s * P * J : (s + count) * P * J, :].rearrange("(s p j) c -> p s (j c)", p=P, j=J)
-                )
-                got.extend(raw[:, i, :].rearrange("p (j c) -> p j c", j=J) for i in range(count))
-            return got[s]
+        def load_pass(rows, pool, tag):
+            raw = pool.tile([P, J, rows.shape[1]], F32, name="raw", tag=tag, align_bytes=64)
+            nc.sync.dma_start(out=raw[:], in_=rows.rearrange("(p j) c -> p j c", j=J))
+            return raw[:]
 
-        def shared_copy(dst, src, cut):
-            if cut > 0:
-                nc.vector.tensor_copy(out=dst[:, :cut], in_=src[:, :cut])
-            if cut < dst.shape[1]:
-                nc.scalar.activation(dst[:, cut:], src[:, cut:], COPY)
+        def shared_copy(dst, src, share):
+            nc.vector.tensor_copy(out=dst[:, :share], in_=src[:, :share])
+            nc.scalar.activation(dst[:, share:], src[:, share:], COPY)
+
+        def interleaved(rows, grouped):
+            return grouped.rearrange("p (c i) j -> p c j i", i=4), rows.rearrange("p j (c i) -> p c j i", i=4)
+
+        def quantise(words, scales, values):
+            nc.vector.quantize_mx(out=words.bitcast(FP8X4), scales=scales, in_=values)
+
+        def matmul(acc, lhs_words, lhs_scales, rhs_words, rhs_scales, start, stop):
+            nc.tensor.matmul_mx(
+                out=acc,
+                lhsT=lhs_words.bitcast(FP8X4),
+                lhsT_scale=lhs_scales,
+                rhs=rhs_words.bitcast(FP8X4),
+                rhs_scale=rhs_scales,
+                start=start,
+                stop=stop,
+            )
 
         x_scales = keep.tile([P, T], U8, name="x_scales", align_bytes=64)
         nc.gpsimd.memset(x_scales[:], 0)
         offsets = keep.tile([P, TOP * T // 16], U16, name="offsets")
         x_words = []
-        got = []
         for s in range(S):
             if s == S // 2:
                 nc.sync.dma_start(offsets[:], offs)
-            raw = load(xT, s, X_LOADS, got)
-            grouped = groups.tile([P, T, J], BF16, name="xg", tag="grouped", align_bytes=64)
-            shared_copy(
-                grouped[:].rearrange("p (c i) j -> p c j i", i=4), raw.rearrange("p j (c i) -> p c j i", i=4), X_SHARE[s]
-            )
+            raw = load_pass(xT[s * P * J : (s + 1) * P * J, :], stage, "raw")
+            grouped = groups.tile([P, T, J], BF16, name="x_grouped", tag="grouped", align_bytes=64)
+            shared_copy(*interleaved(raw, grouped[:]), X_SHARE)
             words = keep.tile([P, T], U32, name=f"x_words{s}", align_bytes=64)
-            nc.vector.quantize_mx(
-                out=words[:].bitcast(FP8X4),
-                scales=x_scales[4 * s :, :],
-                in_=grouped[:].rearrange("p t j -> p (t j)"),
-            )
+            quantise(words[:], x_scales[SCALE_ROWS * s :, :], grouped[:].rearrange("p t j -> p (t j)"))
             x_words.append(words)
 
-        y = keep.tile([P, E * C], F32, name="y", align_bytes=64)
-
         def gather(e):
-            words = keep.tile([P, S, C], U32, name="slot_words", tag=f"words{e}", align_bytes=64)
-            scales = keep.tile([P, C], U8, name="slot_scales", tag=f"scales{e}", align_bytes=64)
+            words = keep.tile([P, S, C], U32, name="slot_words", tag=f"slot_words{e}", align_bytes=64)
+            scales = keep.tile([P, C], U8, name="slot_scales", tag=f"slot_scales{e}", align_bytes=64)
             where = offsets[:, e * LIST : (e + 1) * LIST]
             for s in range(S):
                 nc.vector.tensor_copy(words[:, s, :], x_words[s][:].indirect(where))
             nc.vector.tensor_copy(scales[:], x_scales[:].indirect(where))
             return words, scales
 
-        lent = {QHOLD[e]: f"h_words{e}" for e in QHOLD}
-        for e in GHOLD:
-            lent[GHOLD[e][0]] = f"words{e}"
-            lent[GHOLD[e][1]] = f"scales{e}"
+        lent = {}
+        for e in range(EARLY_EXPERTS, E):
+            lent[(e - GATHER_AHEAD, GATHER_WORDS_AT)] = f"slot_words{e}"
+            lent[(e - GATHER_AHEAD, GATHER_SCALES_AT)] = f"slot_scales{e}"
 
-        def chunk(raw, k, cut, step):
-            if k in lent:
-                grouped = keep.tile([P, H, J], BF16, name="wg", tag=lent[k], align_bytes=64)
-            else:
-                grouped = groups.tile([P, H, J], BF16, name="wg", tag="grouped", align_bytes=64)
-            dst = grouped[:].rearrange("p (t m) j -> p m j t", t=HT)
-            if raw is None:
-                m0 = 0
-                for width, share in LAST_PIECES:
-                    piece = stage.tile([P, J, width * HT], F32, name="raw", tag="raw", align_bytes=64)
-                    rows = w1[E - 1, (S - 1) * P * J :, m0 * HT : (m0 + width) * HT]
-                    nc.sync.dma_start(out=piece[:], in_=rows.rearrange("(p j) c -> p j c", j=J))
-                    shared_copy(dst[:, m0 : m0 + width], piece[:].rearrange("p j (m t) -> p m j t", t=HT), share)
-                    m0 = m0 + width
-            else:
-                shared_copy(dst, raw.rearrange("p j (m t) -> p m j t", t=HT), cut)
+        def quantise_chunk(raw, e, s, share, step):
+            pool, tag = (keep, lent[(e, s)]) if (e, s) in lent else (groups, "grouped")
+            grouped = pool.tile([P, H, J], BF16, name="w1_grouped", tag=tag, align_bytes=64)
+            shared_copy(
+                grouped[:].rearrange("p (t m) j -> p m j t", t=HT), raw.rearrange("p j (m t) -> p m j t", t=HT), share
+            )
             words = codes.tile([P, H], U32, name="w1_words", align_bytes=64)
             scales = codes.tile([P, H], U8, name="w1_scales", align_bytes=64)
             for lo in range(0, H, step):
-                nc.vector.quantize_mx(
-                    out=words[:, lo : lo + step].bitcast(FP8X4),
-                    scales=scales[:, lo : lo + step],
-                    in_=grouped[:, lo : lo + step, :].rearrange("p h j -> p (h j)"),
-                )
+                values = grouped[:, lo : lo + step, :].rearrange("p h j -> p (h j)")
+                quantise(words[:, lo : lo + step], scales[:, lo : lo + step], values)
             return words, scales
 
-        second_w = {}
-
-        def second_load(e0, e1):
-            raw = stage.tile([P, e1 - e0, J * N], F32, name="raw", tag="raw", align_bytes=64)
-            nc.sync.dma_start(out=raw[:], in_=w2[e0:e1].rearrange("e (p j) n -> p e (j n)", j=J))
-            return raw
-
-        def second_weights(raw, e0, e1, eng):
-            if e1 - e0 > 1 and W2_SPLIT:
-                for e in range(e0, e1):
-                    second_weights(raw[:, e - e0 : e - e0 + 1, :], e, e + 1, eng[e - e0])
-                    if W2_SPLIT > 1:
-                        finish(e)
-                return
-            grouped = groups.tile([P, e1 - e0, N, J], BF16, name="w2g", tag="grouped", align_bytes=64)
-            for e in range(e1 - e0):
-                shared_copy(
-                    grouped[:, e].rearrange("p (c i) j -> p c j i", i=4),
-                    raw[:, e, :].rearrange("p (j c i) -> p c j i", j=J, i=4),
-                    eng[e] if isinstance(eng[e], int) else (32 if eng[e] == "v" else 0),
-                )
-            words = keep.tile([P, e1 - e0, N], U32, name=f"w2_words{e0}", align_bytes=64)
-            scales = keep.tile([P, e1 - e0, N], U8, name=f"w2_scales{e0}", align_bytes=64)
-            nc.vector.quantize_mx(
-                out=words[:].rearrange("p e n -> p (e n)").bitcast(FP8X4),
-                scales=scales[:].rearrange("p e n -> p (e n)"),
-                in_=grouped[:].rearrange("p e n j -> p (e n j)"),
-            )
-            for e in range(e0, e1):
-                second_w[e] = (words[:, e - e0, :], scales[:, e - e0, :])
-
-        def second(e, lo, hi, eng):
-            acc = psum.tile([P, C], F32, name="y_acc", tag="bank")
-            words, scales = hidden[e]
-            nc.tensor.matmul_mx(
-                out=acc[:, : hi - lo],
-                lhsT=second_w[e][0].bitcast(FP8X4),
-                lhsT_scale=second_w[e][1],
-                rhs=words[:, lo:hi].bitcast(FP8X4),
-                rhs_scale=scales[:, lo:hi],
-                start=True,
-                stop=True,
-            )
-            copy_out = nc.vector.tensor_copy if eng == "v" else nc.scalar.copy
-            copy_out(y[:, e * C + lo : e * C + hi], acc[:, : hi - lo])
-
-        def product(acc, weights, t, slots, s, lo, hi):
-            nc.tensor.matmul_mx(
-                out=acc,
-                lhsT=weights[0][:, t * M : (t + 1) * M].bitcast(FP8X4),
-                lhsT_scale=weights[1][:, t * M : (t + 1) * M],
-                rhs=slots[0][:, s, lo:hi].bitcast(FP8X4),
-                rhs_scale=slots[1][4 * s :, lo:hi],
-                start=s == 0,
-                stop=s == S - 1,
+        def first_product(acc, chunk, t, e, s, lo, hi):
+            cols = slice(t * M, (t + 1) * M)
+            words, scales = slots[e]
+            matmul(
+                acc, chunk[0][:, cols], chunk[1][:, cols], words[:, s, lo:hi], scales[SCALE_ROWS * s :, lo:hi],
+                s == 0, s == S - 1,
             )
 
-        def quantise_hidden(e, pieces):
-            h_words = keep.tile([P, C], U32, name=f"h_words{e}", tag=f"h_words{e}", align_bytes=64)
-            h_scales = keep.tile([P, C], U8, name=f"h_scales{e}", align_bytes=64)
-            hidden[e] = (h_words, h_scales)
-            width = C // len(pieces)
-            for i, piece in enumerate(pieces):
-                nc.vector.quantize_mx(
-                    out=h_words[:, i * width : (i + 1) * width].bitcast(FP8X4),
-                    scales=h_scales[:, i * width : (i + 1) * width],
-                    in_=piece,
-                )
+        def quantise_hidden(e, halves):
+            words = keep.tile([P, C], U32, name=f"h_words{e}", align_bytes=64)
+            scales = keep.tile([P, C], U8, name=f"h_scales{e}", align_bytes=64)
+            for (lo, hi), half in zip(HALVES, halves):
+                quantise(words[:, lo:hi], scales[:, lo:hi], half)
+            hidden.append((words, scales))
 
-        def first_layer(weights, slots):
-            banks = []
-            for lo, hi in parts:
-                bank = psum.tile([P, HT, HALF], F32, name="h_acc", tag="bank")
-                for t in range(HT):
-                    for s in range(S):
-                        product(bank[:, t, :], weights[s], t, slots, s, lo, hi)
-                banks.append(bank)
-            return banks
-
-        def hidden_out(e, banks, raw):
-            if S_ONLY:
-                halves = [raw[:, i, H // 2 :].bitcast(BF16) for i in range(2)]
-            else:
-                halves = [raw[:, 0, i * H // 2 : (i + 1) * H // 2].bitcast(BF16) for i in range(2)]
-            for half, bank in zip(halves, banks):
-                nc.scalar.activation(
-                    half.rearrange("p (c t) -> p c t", t=HT), bank[:].rearrange("p t c -> p c t"), RELU
-                )
-            return halves if S_ONLY else [raw[:, 0, :].bitcast(BF16)]
-
-        def finish(d):
-            if d == E - 1:
-                for i, (lo, hi) in enumerate(parts):
-                    second(d, lo, hi, YCOPY[d + i])
-            else:
-                second(d, 0, C, YCOPY[d])
-
-        hidden = {}
-        parts = [(0, HALF), (HALF, C)]
-        slots = {e: gather(e) for e in range(E) if e not in GHOLD}
-        banks = None
+        hidden = []
+        slots = [gather(e) for e in range(EARLY_EXPERTS)]
+        h_banks = []
         for e in range(E):
             last = e == E - 1
-            weights = []
-            got = []
-            if last and not LAST_FUSED:
-                tiles = [psum.tile([P, C], F32, name="h_acc", tag="bank") for t in range(HT)]
+            hidden_at = HIDDEN_AT - 1 if last else HIDDEN_AT
+            chunks = []
+            if last:
+                tile_banks = [psum.tile([P, C], F32, name="tile_bank", tag="bank") for t in range(HT)]
             for s in range(S):
-                raw = None if last and s == S - 1 else load(w1[e], s, LOADS[e], got)
-                weights.append(chunk(raw, e * S + s, SHARE[e][s], QSTEP if last and s == S - 1 else H))
-                if last and not LAST_FUSED:
+                raw = load_pass(w1[e, s * P * J : (s + 1) * P * J, :], stage, "raw")
+                share = SHARE_WHILE_GATHERING if e + GATHER_AHEAD < E else SHARE_AFTER
+                if s == hidden_at:
+                    share = min(share, M // 2)
+                chunks.append(quantise_chunk(raw, e, s, share, M if last and s == S - 1 else H))
+                if last:
                     for t in range(HT):
-                        product(tiles[t][:], weights[s], t, slots[e], s, 0, C)
-                if s == HOLD[e] and e > 0:
-                    waiting = hidden_out(e - 1, banks, raw)
-                    if e - 1 not in QHOLD:
-                        quantise_hidden(e - 1, waiting)
-                for d in QHOLD:
-                    if QHOLD[d] == e * S + s:
-                        quantise_hidden(d, waiting)
-                for d in GHOLD:
-                    if max(GHOLD[d]) == e * S + s:
-                        slots[d] = gather(d)
-                if e * S + s == EARLY_AT:
-                    for e0, e1, eng in W2_EARLY:
-                        second_weights(second_load(e0, e1), e0, e1, eng)
-                if e * S + s == EARLY_AT + 1:
-                    for e0, e1, eng in W2_EARLY:
-                        for d in range(e0, min(e1, E - 1)):
-                            second(d, 0, C, YCOPY[d])
+                        first_product(tile_banks[t][:], chunks[s], t, e, s, 0, C)
+                if s == hidden_at and e > 0:
+                    halves = [raw[:, i, H // 2 :].bitcast(BF16) for i in range(len(HALVES))]
+                    for half, bank in zip(halves, h_banks):
+                        nc.scalar.activation(
+                            half.rearrange("p (c t) -> p c t", t=HT), bank[:].rearrange("p t c -> p c t"), RELU
+                        )
+                    quantise_hidden(e - 1, halves)
+                if s == GATHER_SCALES_AT and EARLY_EXPERTS <= e + GATHER_AHEAD < E:
+                    slots.append(gather(e + GATHER_AHEAD))
             if not last:
-                banks = first_layer(weights, slots[e])
+                h_banks = []
+                for lo, hi in HALVES:
+                    bank = psum.tile([P, HT, HALF], F32, name="h_bank", tag="bank")
+                    for t in range(HT):
+                        for s in range(S):
+                            first_product(bank[:, t, :], chunks[s], t, e, s, lo, hi)
+                    h_banks.append(bank)
 
-        e = E - 1
-        raws = [second_load(e0, e1) for e0, e1, eng in W2_LATE]
+        w2_raw = [load_pass(w2[e], *((keep, "y") if e == E - 1 else (stage, "raw"))) for e in range(E)]
+        y = keep.tile([P, E * C], F32, name="y", tag="y", align_bytes=64)
+
         h_grouped = keep.tile([P, C, HT], BF16, name="h_grouped", align_bytes=64)
         h_rows = keep.tile([P, HT, C], BF16, name="h_rows", align_bytes=64)
         for t in range(HT):
-            if t in RELU_V:
-                nc.vector.tensor_scalar_max(h_rows[:, t, :], tiles[t][:], 0.0)
+            nc.scalar.activation(h_rows[:, t, :], tile_banks[t][:], RELU)
+
+        w2_codes = []
+        for e in range(E):
+            grouped = groups.tile([P, N, J], BF16, name="w2_grouped", tag="grouped", align_bytes=64)
+            dst, src = interleaved(w2_raw[e], grouped[:])
+            if e in W2_ON_VECTOR:
+                nc.vector.tensor_copy(out=dst, in_=src)
             else:
-                nc.scalar.activation(h_rows[:, t, :], tiles[t][:], RELU)
+                nc.scalar.activation(dst, src, COPY)
+            words = keep.tile([P, N], U32, name=f"w2_words{e}", align_bytes=64)
+            scales = keep.tile([P, N], U8, name=f"w2_scales{e}", align_bytes=64)
+            quantise(words[:], scales[:], grouped[:].rearrange("p n j -> p (n j)"))
+            w2_codes.append((words, scales))
 
-        def last_hidden():
-            for lo, hi in parts:
-                nc.vector.tensor_copy(
-                    out=h_grouped[:, lo:hi, :].rearrange("p (c i) t -> p c t i", i=4),
-                    in_=h_rows[:, :, lo:hi].rearrange("p t (c i) -> p c t i", i=4),
-                )
-            quantise_hidden(e, [h_grouped[:, lo:hi, :].rearrange("p c t -> p (c t)") for lo, hi in parts])
+        for lo, hi in HALVES:
+            dst, src = interleaved(h_rows[:, :, lo:hi], h_grouped[:, lo:hi, :])
+            nc.vector.tensor_copy(out=dst, in_=src)
+        quantise_hidden(E - 1, [h_grouped[:, lo:hi, :].rearrange("p c t -> p (c t)") for lo, hi in HALVES])
 
-        for i, (raw, (e0, e1, eng)) in enumerate(zip(raws, W2_LATE)):
-            if i == H_AT:
-                last_hidden()
-            second_weights(raw, e0, e1, eng)
-            if not FINISH_LATE:
-                finish(e0)
-        if H_AT == len(raws):
-            last_hidden()
-        if FINISH_LATE:
-            for e0, e1, eng in W2_LATE:
-                finish(e0)
+        pieces = [(e, 0, C) for e in range(E - 1)] + [(E - 1, lo, hi) for lo, hi in HALVES]
+        for i, (e, lo, hi) in enumerate(pieces):
+            acc = psum.tile([P, C], F32, name="y_bank", tag="bank")
+            matmul(
+                acc[:, : hi - lo], w2_codes[e][0][:], w2_codes[e][1][:], hidden[e][0][:, lo:hi], hidden[e][1][:, lo:hi],
+                True, True,
+            )
+            copy_out = nc.scalar.copy if i % 2 == 0 else nc.vector.tensor_copy
+            copy_out(y[:, e * C + lo : e * C + hi], acc[:, : hi - lo])
+
         places = []
         for r, pos in enumerate((pos1, pos2, pos3)):
             place = keep.tile([P, T // 16], U16, name=f"place{r}")
             nc.sync.dma_start(place[:], pos)
             places.append(place)
-        gate_tile = stage.tile([P, TOP, T], F32, name="raw", tag="raw", align_bytes=64)
-        gates = [gate_tile[:, r, :] for r in range(TOP)]
+        gates = stage.tile([P, TOP, T], F32, name="gates", tag="raw", align_bytes=64)
         for r in range(TOP):
-            nc.sync.dma_start(out=gates[r], in_=gate[r])
+            nc.sync.dma_start(out=gates[:, r, :], in_=gate[r])
 
         products = []
         for r in range(TOP):
             scaled = keep.tile([P, T], F32, name=f"scaled{r}", align_bytes=64)
-            nc.vector.tensor_tensor(scaled[:], y[:].indirect(places[r][:]), gates[r], MULT)
+            nc.vector.tensor_tensor(scaled[:], y[:].indirect(places[r][:]), gates[:, r, :], MULT)
             products.append(scaled)
         pair = keep.tile([P, T], F32, name="pair", align_bytes=64)
         total = keep.tile([P, T], F32, name="total", align_bytes=64)
-        halves = [slice(0, CUT), slice(CUT, T)]
-        for cols in halves:
+        token_halves = [slice(0, T // 2), slice(T // 2, T)]
+        for cols in token_halves:
             nc.vector.tensor_tensor(pair[:, cols], products[0][:, cols], products[1][:, cols], ADD)
-        for cols in halves:
+        for cols in token_halves:
             nc.vector.tensor_tensor(total[:, cols], pair[:, cols], products[2][:, cols], ADD)
             nc.sync.dma_start(out=out[:, cols], in_=total[:, cols])

@@ -37,6 +37,7 @@ GATHER_SCALES_AT = 3
 HIDDEN_AT = 2
 W2_ON_VECTOR = range(2, 4)
 
+DMA_ALIGN = 256
 STAGE_BUFS = 11
 GROUPED_BUFS = 5
 CODE_BUFS = 2 * S
@@ -52,7 +53,7 @@ def tile_moe_tk_mlp_relu_kernel(tc, xT, w1, w2, gate, offs, pos1, pos2, pos3, ou
         psum = ctx.enter_context(tc.psum_pool(name="psum", bufs=8))
 
         def load_pass(rows, pool, tag):
-            raw = pool.tile([P, J, rows.shape[1]], F32, name="raw", tag=tag, align_bytes=64)
+            raw = pool.tile([P, J, rows.shape[1]], F32, name="raw", tag=tag, align_bytes=DMA_ALIGN)
             nc.sync.dma_start(out=raw[:], in_=rows.rearrange("(p j) c -> p j c", j=J))
             return raw[:]
 
@@ -170,7 +171,7 @@ def tile_moe_tk_mlp_relu_kernel(tc, xT, w1, w2, gate, offs, pos1, pos2, pos3, ou
                     h_banks.append(bank)
 
         w2_raw = [load_pass(w2[e], *((keep, "y") if e == E - 1 else (stage, "raw"))) for e in range(E)]
-        y = keep.tile([P, E * C], F32, name="y", tag="y", align_bytes=64)
+        y = keep.tile([P, E * C], F32, name="y", tag="y", align_bytes=DMA_ALIGN)
 
         h_grouped = keep.tile([P, C, HT], BF16, name="h_grouped", align_bytes=64)
         h_rows = keep.tile([P, HT, C], BF16, name="h_rows", align_bytes=64)
@@ -210,7 +211,7 @@ def tile_moe_tk_mlp_relu_kernel(tc, xT, w1, w2, gate, offs, pos1, pos2, pos3, ou
             place = keep.tile([P, T // 16], U16, name=f"place{r}")
             nc.sync.dma_start(place[:], pos)
             places.append(place)
-        gates = stage.tile([P, TOP, T], F32, name="gates", tag="raw", align_bytes=64)
+        gates = stage.tile([P, TOP, T], F32, name="gates", tag="raw", align_bytes=DMA_ALIGN)
         for r in range(TOP):
             nc.sync.dma_start(out=gates[:, r, :], in_=gate[r])
 
@@ -220,7 +221,7 @@ def tile_moe_tk_mlp_relu_kernel(tc, xT, w1, w2, gate, offs, pos1, pos2, pos3, ou
             nc.vector.tensor_tensor(scaled[:], y[:].indirect(places[r][:]), gates[:, r, :], MULT)
             products.append(scaled)
         pair = keep.tile([P, T], F32, name="pair", align_bytes=64)
-        total = keep.tile([P, T], F32, name="total", align_bytes=64)
+        total = keep.tile([P, T], F32, name="total", align_bytes=DMA_ALIGN)
         token_halves = [slice(0, T // 2), slice(T // 2, T)]
         for cols in token_halves:
             nc.vector.tensor_tensor(pair[:, cols], products[0][:, cols], products[1][:, cols], ADD)

@@ -29,12 +29,14 @@ SCALE_ROWS = 4
 
 X_SHARE = 16
 SHARE_WHILE_GATHERING = 40
-SHARE_AFTER = 84
+SHARE_AFTER = 64
+SHARE_LAST = 84
 EARLY_EXPERTS = 3
 GATHER_AHEAD = 2
 GATHER_WORDS_AT = 1
 GATHER_SCALES_AT = 3
 HIDDEN_AT = 2
+PASS_BY_PASS = E - 2
 W2_ON_VECTOR = range(2, 4)
 
 DMA_ALIGN = 256
@@ -134,25 +136,39 @@ def tile_moe_tk_mlp_relu_kernel(tc, xT, w1, w2, gate, offs, pos1, pos2, pos3, ou
                 quantise(words[:, lo:hi], scales[:, lo:hi], half)
             hidden.append((words, scales))
 
+        def rows_out(rows, banks):
+            for t in range(HT):
+                nc.scalar.activation(rows[:, t, :], banks[t][:], RELU)
+
+        def interleave_hidden(e, rows):
+            grouped = keep.tile([P, C, HT], BF16, name=f"h_grouped{e}", align_bytes=64)
+            for lo, hi in HALVES:
+                dst, src = interleaved(rows[:, :, lo:hi], grouped[:, lo:hi, :])
+                nc.vector.tensor_copy(out=dst, in_=src)
+            quantise_hidden(e, [grouped[:, lo:hi, :].rearrange("p c t -> p (c t)") for lo, hi in HALVES])
+
         hidden = []
         slots = [gather(e) for e in range(EARLY_EXPERTS)]
         h_banks = []
         for e in range(E):
             last = e == E - 1
-            hidden_at = HIDDEN_AT - 1 if last else HIDDEN_AT
             chunks = []
-            if last:
+            if e >= PASS_BY_PASS:
                 tile_banks = [psum.tile([P, C], F32, name="tile_bank", tag="bank") for t in range(HT)]
             for s in range(S):
                 raw = load_pass(w1[e, s * P * J : (s + 1) * P * J, :], stage, "raw")
                 share = SHARE_WHILE_GATHERING if e + GATHER_AHEAD < E else SHARE_AFTER
-                if s == hidden_at:
-                    share = min(share, M // 2)
+                if last and s == S - 1:
+                    share = SHARE_LAST
                 chunks.append(quantise_chunk(raw, e, s, share, M if last and s == S - 1 else H))
-                if last:
+                if e >= PASS_BY_PASS:
                     for t in range(HT):
                         first_product(tile_banks[t][:], chunks[s], t, e, s, 0, C)
-                if s == hidden_at and e > 0:
+                if s == 0 and e > PASS_BY_PASS:
+                    rows = raw[:, :, H - C // 2 :].bitcast(BF16)
+                    rows_out(rows, h_banks)
+                    interleave_hidden(e - 1, rows)
+                if s == HIDDEN_AT and 0 < e <= PASS_BY_PASS:
                     halves = [raw[:, i, H // 2 :].bitcast(BF16) for i in range(len(HALVES))]
                     for half, bank in zip(halves, h_banks):
                         nc.scalar.activation(
@@ -161,7 +177,9 @@ def tile_moe_tk_mlp_relu_kernel(tc, xT, w1, w2, gate, offs, pos1, pos2, pos3, ou
                     quantise_hidden(e - 1, halves)
                 if s == GATHER_SCALES_AT and EARLY_EXPERTS <= e + GATHER_AHEAD < E:
                     slots.append(gather(e + GATHER_AHEAD))
-            if not last:
+            if e >= PASS_BY_PASS:
+                h_banks = tile_banks
+            else:
                 h_banks = []
                 for lo, hi in HALVES:
                     bank = psum.tile([P, HT, HALF], F32, name="h_bank", tag="bank")
@@ -173,10 +191,8 @@ def tile_moe_tk_mlp_relu_kernel(tc, xT, w1, w2, gate, offs, pos1, pos2, pos3, ou
         w2_raw = [load_pass(w2[e], *((keep, "y") if e == E - 1 else (stage, "raw"))) for e in range(E)]
         y = keep.tile([P, E * C], F32, name="y", tag="y", align_bytes=DMA_ALIGN)
 
-        h_grouped = keep.tile([P, C, HT], BF16, name="h_grouped", align_bytes=64)
         h_rows = keep.tile([P, HT, C], BF16, name="h_rows", align_bytes=64)
-        for t in range(HT):
-            nc.scalar.activation(h_rows[:, t, :], tile_banks[t][:], RELU)
+        rows_out(h_rows[:], h_banks)
 
         w2_codes = []
         for e in range(E):
@@ -191,10 +207,7 @@ def tile_moe_tk_mlp_relu_kernel(tc, xT, w1, w2, gate, offs, pos1, pos2, pos3, ou
             quantise(words[:], scales[:], grouped[:].rearrange("p n j -> p (n j)"))
             w2_codes.append((words, scales))
 
-        for lo, hi in HALVES:
-            dst, src = interleaved(h_rows[:, :, lo:hi], h_grouped[:, lo:hi, :])
-            nc.vector.tensor_copy(out=dst, in_=src)
-        quantise_hidden(E - 1, [h_grouped[:, lo:hi, :].rearrange("p c t -> p (c t)") for lo, hi in HALVES])
+        interleave_hidden(E - 1, h_rows[:])
 
         pieces = [(e, 0, C) for e in range(E - 1)] + [(E - 1, lo, hi) for lo, hi in HALVES]
         for i, (e, lo, hi) in enumerate(pieces):

@@ -1,6 +1,7 @@
 from contextlib import ExitStack
 
 import concourse.mybir as mybir
+from concourse.masks import make_identity
 
 K, T, E, C, H, N, TOP = 2048, 512, 6, 256, 512, 128, 3
 
@@ -82,6 +83,8 @@ def tile_moe_tk_mlp_relu_kernel(tc, xT, w1, w2, gate, offs, pos1, pos2, pos3, ou
 
         x_scales = keep.tile([P, T], U8, name="x_scales", align_bytes=64)
         nc.gpsimd.memset(x_scales[:], 0)
+        identity = keep.tile([P, P], F32, name="identity", align_bytes=64)
+        make_identity(nc, identity[:])
         offsets = keep.tile([P, TOP * T // 16], U16, name="offsets")
         x_words = []
         for s in range(S):
@@ -225,19 +228,36 @@ def tile_moe_tk_mlp_relu_kernel(tc, xT, w1, w2, gate, offs, pos1, pos2, pos3, ou
             nc.sync.dma_start(place[:], pos)
             places.append(place)
         gates = stage.tile([P, TOP, T], F32, name="gates", tag="raw", align_bytes=DMA_ALIGN)
-        for r in range(TOP):
-            nc.sync.dma_start(out=gates[:, r, :], in_=gate[r])
+        nc.sync.dma_start(out=gates[:, :2, :], in_=gate[:2].rearrange("r p t -> p r t"))
+        nc.sync.dma_start(out=gates[:, 2, :], in_=gate[2])
 
-        products = []
-        for r in range(TOP):
-            scaled = keep.tile([P, T], F32, name=f"scaled{r}", align_bytes=64)
-            nc.vector.tensor_tensor(scaled[:], y[:].indirect(places[r][:]), gates[:, r, :], MULT)
-            products.append(scaled)
-        pair = keep.tile([P, T], F32, name="pair", align_bytes=64)
-        total = keep.tile([P, T], F32, name="total", align_bytes=DMA_ALIGN)
+        products = [keep.tile([P, T], F32, name=f"scaled{r}", align_bytes=64) for r in range(TOP)]
+
+        def gather_times_gate(r, cols):
+            where = places[r][:, cols.start // 16 : cols.stop // 16]
+            nc.vector.tensor_tensor(products[r][:, cols], y[:].indirect(where), gates[:, r, cols], MULT)
+
+        summed = []
+        for part in (slice(0, T - P), slice(T - P, T)):
+            token_tiles = [slice(lo, lo + P) for lo in range(part.start, part.stop, P)]
+            turned = [psum.tile([P, P], F32, name="turned", tag="bank") for cols in token_tiles]
+            for r in range(2):
+                gather_times_gate(r, part)
+                for bank, cols in zip(turned, token_tiles):
+                    nc.tensor.matmul(
+                        bank[:], products[r][:, cols], identity[:], start=r == 0, stop=r == 1, is_transpose=True
+                    )
+            for bank, cols in zip(turned, token_tiles):
+                rows = keep.tile([P, P], F32, name=f"summed{cols.start}", align_bytes=64)
+                nc.scalar.copy(rows[:], bank[:])
+                summed.append(rows)
         token_halves = [slice(0, T // 2), slice(T // 2, T)]
         for cols in token_halves:
-            nc.vector.tensor_tensor(pair[:, cols], products[0][:, cols], products[1][:, cols], ADD)
-        for cols in token_halves:
-            nc.vector.tensor_tensor(total[:, cols], pair[:, cols], products[2][:, cols], ADD)
+            gather_times_gate(2, cols)
+        pairs = [psum.tile([P, T // 2], F32, name="pair", tag="bank") for cols in token_halves]
+        for i, rows in enumerate(summed):
+            nc.tensor.transpose(pairs[i // 2][:, i % 2 * P : (i % 2 + 1) * P], rows[:], identity[:])
+        total = keep.tile([P, T], F32, name="total", align_bytes=DMA_ALIGN)
+        for cols, pair in zip(token_halves, pairs):
+            nc.vector.tensor_tensor(total[:, cols], products[2][:, cols], pair[:], ADD)
             nc.sync.dma_start(out=out[:, cols], in_=total[:, cols])

@@ -30,19 +30,21 @@ SCALE_ROWS = 4
 
 X_SHARE = 16
 SHARE_WHILE_GATHERING = 40
-SHARE_AFTER = 64
+SHARE_CATCHING_UP = 56
 SHARE_LAST = 84
-EARLY_EXPERTS = 3
+GATHER = 384
+VECTOR_FROM = 7
 GATHER_AHEAD = 2
 GATHER_WORDS_AT = 1
 GATHER_SCALES_AT = 3
 HIDDEN_AT = 2
-PASS_BY_PASS = E - 2
-W2_ON_VECTOR = range(2, 4)
+PASS_BY_PASS = 2
+W2_ON_VECTOR = range(3, 5)
+W2_LAST_SHARE = 20
 
 DMA_ALIGN = 256
 STAGE_BUFS = 11
-GROUPED_BUFS = 5
+GROUPED_BUFS = 8
 CODE_BUFS = 2 * S
 
 
@@ -61,8 +63,10 @@ def tile_moe_tk_mlp_relu_kernel(tc, xT, w1, w2, gate, offs, pos1, pos2, pos3, ou
             return raw[:]
 
         def shared_copy(dst, src, share):
-            nc.vector.tensor_copy(out=dst[:, :share], in_=src[:, :share])
-            nc.scalar.activation(dst[:, share:], src[:, share:], COPY)
+            if share > 0:
+                nc.vector.tensor_copy(out=dst[:, :share], in_=src[:, :share])
+            if share < dst.shape[1]:
+                nc.scalar.activation(dst[:, share:], src[:, share:], COPY)
 
         def interleaved(rows, grouped):
             return grouped.rearrange("p (c i) j -> p c j i", i=4), rows.rearrange("p j (c i) -> p c j i", i=4)
@@ -92,28 +96,39 @@ def tile_moe_tk_mlp_relu_kernel(tc, xT, w1, w2, gate, offs, pos1, pos2, pos3, ou
                 nc.sync.dma_start(offsets[:], offs)
             raw = load_pass(xT[s * P * J : (s + 1) * P * J, :], stage, "raw")
             grouped = groups.tile([P, T, J], BF16, name="x_grouped", tag="grouped", align_bytes=64)
-            shared_copy(*interleaved(raw, grouped[:]), X_SHARE)
+            shared_copy(*interleaved(raw, grouped[:]), M if s == 0 else 0)
             words = keep.tile([P, T], U32, name=f"x_words{s}", align_bytes=64)
             quantise(words[:], x_scales[SCALE_ROWS * s :, :], grouped[:].rearrange("p t j -> p (t j)"))
             x_words.append(words)
 
-        def gather(e):
-            words = keep.tile([P, S, C], U32, name="slot_words", tag=f"slot_words{e}", align_bytes=64)
-            scales = keep.tile([P, C], U8, name="slot_scales", tag=f"slot_scales{e}", align_bytes=64)
-            where = offsets[:, e * LIST : (e + 1) * LIST]
-            for s in range(S):
-                nc.vector.tensor_copy(words[:, s, :], x_words[s][:].indirect(where))
-            nc.vector.tensor_copy(scales[:], x_scales[:].indirect(where))
-            return words, scales
+        gate_rows = keep.tile([P, TOP, P], F32, name="gate_rows", align_bytes=DMA_ALIGN)
+        nc.gpsimd.memset(gate_rows[:], 0.0)
+        nc.sync.dma_start(out=gate_rows[: T // P], in_=gate[:, 0, :].rearrange("r (i n) -> i r n", n=P))
+        turned_rows = psum.tile([P, TOP, P], F32, name="turned_rows", tag="bank")
+        for r in range(TOP):
+            nc.tensor.transpose(turned_rows[:, r, :], gate_rows[:, r, :], identity[:])
+        gate_columns = keep.tile([P, TOP, T // P], F32, name="gate_columns", align_bytes=64)
+        nc.scalar.copy(gate_columns[:], turned_rows[:, :, : T // P])
+        gates = keep.tile([P, TOP, T], F32, name="gates", align_bytes=64)
+        for r in range(TOP):
+            spread = psum.tile([P, T], F32, name="spread", tag="bank")
+            for i in range(T // P):
+                column = gate_columns[:, r, i : i + 1].to_broadcast([P, P])
+                nc.tensor.transpose(spread[:, i * P : (i + 1) * P], column, identity[:])
+            nc.scalar.copy(gates[:, r, :], spread[:])
 
-        lent = {}
-        for e in range(EARLY_EXPERTS, E):
-            lent[(e - GATHER_AHEAD, GATHER_WORDS_AT)] = f"slot_words{e}"
-            lent[(e - GATHER_AHEAD, GATHER_SCALES_AT)] = f"slot_scales{e}"
+        def gather(table, dtype, name):
+            picked = keep.tile([P, E * C], dtype, name=name, align_bytes=64)
+            for lo in range(0, E * C, GATHER):
+                where = offsets[:, lo // 16 : (lo + GATHER) // 16]
+                nc.vector.tensor_copy(picked[:, lo : lo + GATHER], table[:].indirect(where))
+            return picked
+
+        slot_words = [gather(x_words[s], U32, f"slot_words{s}") for s in range(S)]
+        slot_scales = gather(x_scales, U8, "slot_scales")
 
         def quantise_chunk(raw, e, s, share, step):
-            pool, tag = (keep, lent[(e, s)]) if (e, s) in lent else (groups, "grouped")
-            grouped = pool.tile([P, H, J], BF16, name="w1_grouped", tag=tag, align_bytes=64)
+            grouped = groups.tile([P, H, J], BF16, name="w1_grouped", tag="grouped", align_bytes=64)
             shared_copy(
                 grouped[:].rearrange("p (t m) j -> p m j t", t=HT), raw.rearrange("p j (m t) -> p m j t", t=HT), share
             )
@@ -124,19 +139,20 @@ def tile_moe_tk_mlp_relu_kernel(tc, xT, w1, w2, gate, offs, pos1, pos2, pos3, ou
                 quantise(words[:, lo : lo + step], scales[:, lo : lo + step], values)
             return words, scales
 
-        def first_product(acc, chunk, t, e, s, lo, hi):
+        def first_product(acc, chunk, t, e, s, lo, hi, opens=True, closes=True):
             cols = slice(t * M, (t + 1) * M)
-            words, scales = slots[e]
+            slots = slice(e * C + lo, e * C + hi)
             matmul(
-                acc, chunk[0][:, cols], chunk[1][:, cols], words[:, s, lo:hi], scales[SCALE_ROWS * s :, lo:hi],
-                s == 0, s == S - 1,
+                acc, chunk[0][:, cols], chunk[1][:, cols], slot_words[s][:, slots], slot_scales[SCALE_ROWS * s :, slots],
+                opens and s == 0, closes and s == S - 1,
             )
 
         def quantise_hidden(e, halves):
             words = keep.tile([P, C], U32, name=f"h_words{e}", align_bytes=64)
             scales = keep.tile([P, C], U8, name=f"h_scales{e}", align_bytes=64)
-            for (lo, hi), half in zip(HALVES, halves):
-                quantise(words[:, lo:hi], scales[:, lo:hi], half)
+            step = C // len(halves)
+            for i, half in enumerate(halves):
+                quantise(words[:, i * step : (i + 1) * step], scales[:, i * step : (i + 1) * step], half)
             hidden.append((words, scales))
 
         def rows_out(rows, banks):
@@ -151,20 +167,25 @@ def tile_moe_tk_mlp_relu_kernel(tc, xT, w1, w2, gate, offs, pos1, pos2, pos3, ou
             quantise_hidden(e, [grouped[:, lo:hi, :].rearrange("p c t -> p (c t)") for lo, hi in HALVES])
 
         hidden = []
-        slots = [gather(e) for e in range(EARLY_EXPERTS)]
         h_banks = []
         for e in range(E):
             last = e == E - 1
             chunks = []
-            if e >= PASS_BY_PASS:
+            if last:
+                tile_banks = [psum.tile([P, HT, HALF], F32, name="h_bank", tag="bank") for half in HALVES]
+            elif e >= PASS_BY_PASS:
                 tile_banks = [psum.tile([P, C], F32, name="tile_bank", tag="bank") for t in range(HT)]
             for s in range(S):
                 raw = load_pass(w1[e, s * P * J : (s + 1) * P * J, :], stage, "raw")
-                share = SHARE_WHILE_GATHERING if e + GATHER_AHEAD < E else SHARE_AFTER
-                if last and s == S - 1:
-                    share = SHARE_LAST
-                chunks.append(quantise_chunk(raw, e, s, share, M if last and s == S - 1 else H))
+                share = M if s % 2 == 1 and e * S + s >= VECTOR_FROM else 0
                 if e >= PASS_BY_PASS:
+                    share = SHARE_LAST if last and s == S - 1 else M // 2 if e >= E - 2 else SHARE_CATCHING_UP
+                chunks.append(quantise_chunk(raw, e, s, share, M if last and s == S - 1 else H))
+                if last:
+                    for bank, (lo, hi), tiles in zip(tile_banks, HALVES, (range(HT), reversed(range(HT)))):
+                        for i, t in enumerate(tiles):
+                            first_product(bank[:, t, :], chunks[s], t, e, s, lo, hi, i == 0, i == HT - 1)
+                elif e >= PASS_BY_PASS:
                     for t in range(HT):
                         first_product(tile_banks[t][:], chunks[s], t, e, s, 0, C)
                 if s == 0 and e > PASS_BY_PASS:
@@ -172,14 +193,14 @@ def tile_moe_tk_mlp_relu_kernel(tc, xT, w1, w2, gate, offs, pos1, pos2, pos3, ou
                     rows_out(rows, h_banks)
                     interleave_hidden(e - 1, rows)
                 if s == HIDDEN_AT and 0 < e <= PASS_BY_PASS:
-                    halves = [raw[:, i, H // 2 :].bitcast(BF16) for i in range(len(HALVES))]
-                    for half, bank in zip(halves, h_banks):
+                    values = raw[:, J - 1, :].bitcast(BF16)
+                    for (lo, hi), bank in zip(HALVES, h_banks):
                         nc.scalar.activation(
-                            half.rearrange("p (c t) -> p c t", t=HT), bank[:].rearrange("p t c -> p c t"), RELU
+                            values[:, lo * HT : hi * HT].rearrange("p (c t) -> p c t", t=HT),
+                            bank[:].rearrange("p t c -> p c t"),
+                            RELU,
                         )
-                    quantise_hidden(e - 1, halves)
-                if s == GATHER_SCALES_AT and EARLY_EXPERTS <= e + GATHER_AHEAD < E:
-                    slots.append(gather(e + GATHER_AHEAD))
+                    quantise_hidden(e - 1, [values])
             if e >= PASS_BY_PASS:
                 h_banks = tile_banks
             else:
@@ -194,23 +215,31 @@ def tile_moe_tk_mlp_relu_kernel(tc, xT, w1, w2, gate, offs, pos1, pos2, pos3, ou
         w2_raw = [load_pass(w2[e], *((keep, "y") if e == E - 1 else (stage, "raw"))) for e in range(E)]
         y = keep.tile([P, E * C], F32, name="y", tag="y", align_bytes=DMA_ALIGN)
 
-        h_rows = keep.tile([P, HT, C], BF16, name="h_rows", align_bytes=64)
-        rows_out(h_rows[:], h_banks)
+        h_last = [keep.tile([P, HALF, HT], BF16, name=f"h_last{lo}", align_bytes=64) for lo, hi in HALVES]
+        for half, bank in zip(h_last, h_banks):
+            nc.scalar.activation(half[:], bank[:].rearrange("p t c -> p c t"), RELU)
 
-        w2_codes = []
+        w2_grouped = []
         for e in range(E):
-            grouped = groups.tile([P, N, J], BF16, name="w2_grouped", tag="grouped", align_bytes=64)
+            grouped = keep.tile([P, N, J], BF16, name=f"w2_grouped{e}", align_bytes=64)
             dst, src = interleaved(w2_raw[e], grouped[:])
-            if e in W2_ON_VECTOR:
+            if e == E - 1:
+                shared_copy(dst, src, W2_LAST_SHARE)
+            elif e in W2_ON_VECTOR:
                 nc.vector.tensor_copy(out=dst, in_=src)
             else:
                 nc.scalar.activation(dst, src, COPY)
+            w2_grouped.append(grouped)
+
+        quantise_hidden(E - 1, [half[:].rearrange("p c t -> p (c t)") for half in h_last])
+
+        w2_codes = []
+        for e in range(E):
             words = keep.tile([P, N], U32, name=f"w2_words{e}", align_bytes=64)
             scales = keep.tile([P, N], U8, name=f"w2_scales{e}", align_bytes=64)
-            quantise(words[:], scales[:], grouped[:].rearrange("p n j -> p (n j)"))
+            quantise(words[:], scales[:], w2_grouped[e][:].rearrange("p n j -> p (n j)"))
             w2_codes.append((words, scales))
 
-        interleave_hidden(E - 1, h_rows[:])
 
         pieces = [(e, 0, C) for e in range(E - 1)] + [(E - 1, lo, hi) for lo, hi in HALVES]
         for i, (e, lo, hi) in enumerate(pieces):
@@ -219,17 +248,12 @@ def tile_moe_tk_mlp_relu_kernel(tc, xT, w1, w2, gate, offs, pos1, pos2, pos3, ou
                 acc[:, : hi - lo], w2_codes[e][0][:], w2_codes[e][1][:], hidden[e][0][:, lo:hi], hidden[e][1][:, lo:hi],
                 True, True,
             )
-            copy_out = nc.scalar.copy if i % 2 == 0 else nc.vector.tensor_copy
+            copy_out = nc.vector.tensor_copy if i in (0, 4, 6) else nc.scalar.copy
             copy_out(y[:, e * C + lo : e * C + hi], acc[:, : hi - lo])
 
-        places = []
+        places = [keep.tile([P, T // 16], U16, name=f"place{r}") for r in range(TOP)]
         for r, pos in enumerate((pos1, pos2, pos3)):
-            place = keep.tile([P, T // 16], U16, name=f"place{r}")
-            nc.sync.dma_start(place[:], pos)
-            places.append(place)
-        gates = stage.tile([P, TOP, T], F32, name="gates", tag="raw", align_bytes=DMA_ALIGN)
-        nc.sync.dma_start(out=gates[:, :2, :], in_=gate[:2].rearrange("r p t -> p r t"))
-        nc.sync.dma_start(out=gates[:, 2, :], in_=gate[2])
+            nc.sync.dma_start(places[r][:], pos)
 
         products = [keep.tile([P, T], F32, name=f"scaled{r}", align_bytes=64) for r in range(TOP)]
 

@@ -43,7 +43,7 @@ W2_ON_VECTOR = range(3, 5)
 W2_LAST_SHARE = 20
 
 DMA_ALIGN = 256
-STAGE_BUFS = 11
+STAGE_BUFS = 10
 GROUPED_BUFS = 8
 CODE_BUFS = 2 * S
 
@@ -62,11 +62,14 @@ def tile_moe_tk_mlp_relu_kernel(tc, xT, w1, w2, gate, offs, pos1, pos2, pos3, ou
             nc.sync.dma_start(out=raw[:], in_=rows.rearrange("(p j) c -> p j c", j=J))
             return raw[:]
 
-        def shared_copy(dst, src, share):
+        def shared_copy(dst, src, share, halved=False):
             if share > 0:
                 nc.vector.tensor_copy(out=dst[:, :share], in_=src[:, :share])
             if share < dst.shape[1]:
-                nc.scalar.activation(dst[:, share:], src[:, share:], COPY)
+                middle = (share + dst.shape[1]) // 2 if halved else dst.shape[1]
+                nc.scalar.activation(dst[:, share:middle], src[:, share:middle], COPY)
+                if halved:
+                    nc.scalar.activation(dst[:, middle:], src[:, middle:], COPY)
 
         def interleaved(rows, grouped):
             return grouped.rearrange("p (c i) j -> p c j i", i=4), rows.rearrange("p j (c i) -> p c j i", i=4)
@@ -94,9 +97,13 @@ def tile_moe_tk_mlp_relu_kernel(tc, xT, w1, w2, gate, offs, pos1, pos2, pos3, ou
         for s in range(S):
             if s == S // 2:
                 nc.sync.dma_start(offsets[:], offs)
-            raw = load_pass(xT[s * P * J : (s + 1) * P * J, :], stage, "raw")
+                late_passes = keep.tile([P, S // 2, J, T], F32, name="late_passes", align_bytes=DMA_ALIGN)
+                nc.sync.dma_start(
+                    out=late_passes[:], in_=xT[K // 2 :, :].rearrange("(s p j) c -> p s j c", p=P, j=J)
+                )
+            raw = load_pass(xT[s * P * J : (s + 1) * P * J, :], stage, "raw") if s < S // 2 else late_passes[:, s - S // 2]
             grouped = groups.tile([P, T, J], BF16, name="x_grouped", tag="grouped", align_bytes=64)
-            shared_copy(*interleaved(raw, grouped[:]), M if s == 0 else 0)
+            shared_copy(*interleaved(raw, grouped[:]), M if s == 0 else 0, True)
             words = keep.tile([P, T], U32, name=f"x_words{s}", align_bytes=64)
             quantise(words[:], x_scales[SCALE_ROWS * s :, :], grouped[:].rearrange("p t j -> p (t j)"))
             x_words.append(words)
@@ -130,7 +137,8 @@ def tile_moe_tk_mlp_relu_kernel(tc, xT, w1, w2, gate, offs, pos1, pos2, pos3, ou
         def quantise_chunk(raw, e, s, share, step):
             grouped = groups.tile([P, H, J], BF16, name="w1_grouped", tag="grouped", align_bytes=64)
             shared_copy(
-                grouped[:].rearrange("p (t m) j -> p m j t", t=HT), raw.rearrange("p j (m t) -> p m j t", t=HT), share
+                grouped[:].rearrange("p (t m) j -> p m j t", t=HT), raw.rearrange("p j (m t) -> p m j t", t=HT), share,
+                e < E - 1,
             )
             words = codes.tile([P, H], U32, name="w1_words", align_bytes=64)
             scales = codes.tile([P, H], U8, name="w1_scales", align_bytes=64)

@@ -43,7 +43,7 @@ W2_ON_VECTOR = range(3, 5)
 W2_LAST_SHARE = 20
 
 DMA_ALIGN = 256
-STAGE_BUFS = 10
+STAGE_BUFS = 11
 GROUPED_BUFS = 8
 CODE_BUFS = 2 * S
 
@@ -93,36 +93,36 @@ def tile_moe_tk_mlp_relu_kernel(tc, xT, w1, w2, gate, offs, pos1, pos2, pos3, ou
         identity = keep.tile([P, P], F32, name="identity", align_bytes=64)
         make_identity(nc, identity[:])
         offsets = keep.tile([P, TOP * T // 16], U16, name="offsets")
+        gate_rows = keep.tile([P, P], F32, name="gate_rows", align_bytes=DMA_ALIGN)
+        nc.gpsimd.memset(gate_rows[:], 0.0)
         x_words = []
         for s in range(S):
             if s == S // 2:
                 nc.sync.dma_start(offsets[:], offs)
-                late_passes = keep.tile([P, S // 2, J, T], F32, name="late_passes", align_bytes=DMA_ALIGN)
-                nc.sync.dma_start(
-                    out=late_passes[:], in_=xT[K // 2 :, :].rearrange("(s p j) c -> p s j c", p=P, j=J)
-                )
-            raw = load_pass(xT[s * P * J : (s + 1) * P * J, :], stage, "raw") if s < S // 2 else late_passes[:, s - S // 2]
+            raw = load_pass(xT[s * P * J : (s + 1) * P * J, :], stage, "raw")
+            if s > 0:
+                for h in range(2):
+                    half = gate[s - 1, 0, h * T // 2 : (h + 1) * T // 2].rearrange("(i n) -> i n", n=16)
+                    q = 2 * (s - 1) + h
+                    nc.sync.dma_start(out=gate_rows[:16, 16 * q : 16 * (q + 1)], in_=half)
             grouped = groups.tile([P, T, J], BF16, name="x_grouped", tag="grouped", align_bytes=64)
             shared_copy(*interleaved(raw, grouped[:]), M if s == 0 else 0, True)
             words = keep.tile([P, T], U32, name=f"x_words{s}", align_bytes=64)
             quantise(words[:], x_scales[SCALE_ROWS * s :, :], grouped[:].rearrange("p t j -> p (t j)"))
             x_words.append(words)
 
-        gate_rows = keep.tile([P, TOP, P], F32, name="gate_rows", align_bytes=DMA_ALIGN)
-        nc.gpsimd.memset(gate_rows[:], 0.0)
-        nc.sync.dma_start(out=gate_rows[: T // P], in_=gate[:, 0, :].rearrange("r (i n) -> i r n", n=P))
-        turned_rows = psum.tile([P, TOP, P], F32, name="turned_rows", tag="bank")
-        for r in range(TOP):
-            nc.tensor.transpose(turned_rows[:, r, :], gate_rows[:, r, :], identity[:])
-        gate_columns = keep.tile([P, TOP, T // P], F32, name="gate_columns", align_bytes=64)
-        nc.scalar.copy(gate_columns[:], turned_rows[:, :, : T // P])
+        turned_rows = psum.tile([P, P], F32, name="turned_rows", tag="bank")
+        nc.tensor.transpose(turned_rows[:], gate_rows[:], identity[:])
+        gate_columns = keep.tile([P, 16], F32, name="gate_columns", align_bytes=64)
+        nc.scalar.copy(gate_columns[:], turned_rows[:, :16])
         gates = keep.tile([P, TOP, T], F32, name="gates", align_bytes=64)
-        for r in range(TOP):
-            spread = psum.tile([P, T], F32, name="spread", tag="bank")
-            for i in range(T // P):
-                column = gate_columns[:, r, i : i + 1].to_broadcast([P, P])
-                nc.tensor.transpose(spread[:, i * P : (i + 1) * P], column, identity[:])
-            nc.scalar.copy(gates[:, r, :], spread[:])
+        by_column = gates[:].rearrange("p r (h i n) -> p i (r h) n", h=2, n=16)
+        for b in range(4):
+            spread = psum.tile([P, 4, P // 16, 16], F32, name="spread", tag="bank")
+            for i in range(4):
+                column = gate_columns[:, 4 * b + i : 4 * b + i + 1].to_broadcast([P, P])
+                nc.tensor.transpose(spread[:, i].rearrange("p q n -> p (q n)"), column, identity[:])
+            nc.scalar.copy(by_column[:, 4 * b : 4 * (b + 1)], spread[:, :, : 2 * TOP, :])
 
         def gather(table, dtype, name):
             picked = keep.tile([P, E * C], dtype, name=name, align_bytes=64)
@@ -265,31 +265,45 @@ def tile_moe_tk_mlp_relu_kernel(tc, xT, w1, w2, gate, offs, pos1, pos2, pos3, ou
 
         products = [keep.tile([P, T], F32, name=f"scaled{r}", align_bytes=64) for r in range(TOP)]
 
-        def gather_times_gate(r, cols):
+        def gather_times_gate(product, r, cols):
             where = places[r][:, cols.start // 16 : cols.stop // 16]
-            nc.vector.tensor_tensor(products[r][:, cols], y[:].indirect(where), gates[:, r, cols], MULT)
+            nc.vector.tensor_tensor(product[:, cols], y[:].indirect(where), gates[:, r, cols], MULT)
 
-        summed = []
-        for part in (slice(0, T - P), slice(T - P, T)):
-            token_tiles = [slice(lo, lo + P) for lo in range(part.start, part.stop, P)]
-            turned = [psum.tile([P, P], F32, name="turned", tag="bank") for cols in token_tiles]
-            for r in range(2):
-                gather_times_gate(r, part)
-                for bank, cols in zip(turned, token_tiles):
-                    nc.tensor.matmul(
-                        bank[:], products[r][:, cols], identity[:], start=r == 0, stop=r == 1, is_transpose=True
-                    )
-            for bank, cols in zip(turned, token_tiles):
-                rows = keep.tile([P, P], F32, name=f"summed{cols.start}", align_bytes=64)
-                nc.scalar.copy(rows[:], bank[:])
-                summed.append(rows)
-        token_halves = [slice(0, T // 2), slice(T // 2, T)]
-        for cols in token_halves:
-            gather_times_gate(2, cols)
-        pairs = [psum.tile([P, T // 2], F32, name="pair", tag="bank") for cols in token_halves]
-        for i, rows in enumerate(summed):
-            nc.tensor.transpose(pairs[i // 2][:, i % 2 * P : (i % 2 + 1) * P], rows[:], identity[:])
+        tiles = [slice(lo, lo + P) for lo in range(0, T, P)]
         total = keep.tile([P, T], F32, name="total", align_bytes=DMA_ALIGN)
-        for cols, pair in zip(token_halves, pairs):
-            nc.vector.tensor_tensor(total[:, cols], products[2][:, cols], pair[:], ADD)
-            nc.sync.dma_start(out=out[:, cols], in_=total[:, cols])
+        turned = [psum.tile([P, P], F32, name="turned", tag="bank") for i in range(3)]
+
+        def turn(r, i, stop):
+            nc.tensor.matmul(turned[i][:], products[r][:, tiles[i]], identity[:], start=r == 0, stop=stop, is_transpose=True)
+
+        gather_times_gate(products[0], 0, slice(0, 3 * P))
+        for i in range(3):
+            turn(0, i, False)
+        gather_times_gate(products[1], 1, tiles[0])
+        turn(1, 0, False)
+        gather_times_gate(products[2], 2, tiles[0])
+        turn(2, 0, True)
+        for i in (1, 2):
+            gather_times_gate(products[1], 1, tiles[i])
+            turn(1, i, True)
+        summed = keep.tile([P, 2, P], F32, name="summed", align_bytes=64)
+        sums = []
+        for bank, rows in zip(turned, (summed[:, 0, :], total[:, tiles[3]], summed[:, 1, :])):
+            nc.scalar.copy(rows, bank[:])
+            back = psum.tile([P, P], F32, name="back", tag="bank")
+            nc.tensor.transpose(back[:], rows, identity[:])
+            sums.append(back)
+        nc.scalar.copy(total[:, tiles[0]], sums[0][:])
+        nc.sync.dma_start(out=out[:, tiles[0]], in_=total[:, tiles[0]])
+
+        gather_times_gate(products[2], 2, tiles[1])
+        for r in range(TOP):
+            gather_times_gate(products[r], r, tiles[3])
+        last_pair = keep.tile([P, P], F32, name="last_pair", align_bytes=64)
+        nc.vector.tensor_tensor(last_pair[:], products[0][:, tiles[3]], products[1][:, tiles[3]], ADD)
+        gather_times_gate(products[2], 2, tiles[2])
+        nc.vector.tensor_tensor(total[:, tiles[1]], products[2][:, tiles[1]], sums[1][:], ADD)
+        nc.sync.dma_start(out=out[:, tiles[1]], in_=total[:, tiles[1]])
+        nc.vector.tensor_tensor(total[:, tiles[3]], products[2][:, tiles[3]], last_pair[:], ADD)
+        nc.vector.tensor_tensor(total[:, tiles[2]], products[2][:, tiles[2]], sums[2][:], ADD)
+        nc.sync.dma_start(out=out[:, T // 2 :], in_=total[:, T // 2 :])

@@ -39,8 +39,8 @@ GATHER_WORDS_AT = 1
 GATHER_SCALES_AT = 3
 HIDDEN_AT = 2
 PASS_BY_PASS = 2
-W2_ON_VECTOR = range(3, 5)
-W2_LAST_SHARE = 20
+W2_ON_VECTOR = (0, 3, 4)
+W2_LAST_SHARE = 16
 
 DMA_ALIGN = 256
 STAGE_BUFS = 11
@@ -93,36 +93,32 @@ def tile_moe_tk_mlp_relu_kernel(tc, xT, w1, w2, gate, offs, pos1, pos2, pos3, ou
         identity = keep.tile([P, P], F32, name="identity", align_bytes=64)
         make_identity(nc, identity[:])
         offsets = keep.tile([P, TOP * T // 16], U16, name="offsets")
-        gate_rows = keep.tile([P, P], F32, name="gate_rows", align_bytes=DMA_ALIGN)
-        nc.gpsimd.memset(gate_rows[:], 0.0)
         x_words = []
         for s in range(S):
             if s == S // 2:
                 nc.sync.dma_start(offsets[:], offs)
             raw = load_pass(xT[s * P * J : (s + 1) * P * J, :], stage, "raw")
-            if s > 0:
-                for h in range(2):
-                    half = gate[s - 1, 0, h * T // 2 : (h + 1) * T // 2].rearrange("(i n) -> i n", n=16)
-                    q = 2 * (s - 1) + h
-                    nc.sync.dma_start(out=gate_rows[:16, 16 * q : 16 * (q + 1)], in_=half)
             grouped = groups.tile([P, T, J], BF16, name="x_grouped", tag="grouped", align_bytes=64)
             shared_copy(*interleaved(raw, grouped[:]), M if s == 0 else 0, True)
             words = keep.tile([P, T], U32, name=f"x_words{s}", align_bytes=64)
             quantise(words[:], x_scales[SCALE_ROWS * s :, :], grouped[:].rearrange("p t j -> p (t j)"))
             x_words.append(words)
 
-        turned_rows = psum.tile([P, P], F32, name="turned_rows", tag="bank")
-        nc.tensor.transpose(turned_rows[:], gate_rows[:], identity[:])
-        gate_columns = keep.tile([P, 16], F32, name="gate_columns", align_bytes=64)
-        nc.scalar.copy(gate_columns[:], turned_rows[:, :16])
+        gate_rows = keep.tile([P, TOP, P], F32, name="gate_rows", align_bytes=DMA_ALIGN)
+        nc.gpsimd.memset(gate_rows[:], 0.0)
+        nc.sync.dma_start(out=gate_rows[: T // P], in_=gate[:, 0, :].rearrange("r (i n) -> i r n", n=P))
+        turned_rows = psum.tile([P, TOP, P], F32, name="turned_rows", tag="bank")
+        for r in range(TOP):
+            nc.tensor.transpose(turned_rows[:, r, :], gate_rows[:, r, :], identity[:])
+        gate_columns = keep.tile([P, TOP, T // P], F32, name="gate_columns", align_bytes=64)
+        nc.scalar.copy(gate_columns[:], turned_rows[:, :, : T // P])
         gates = keep.tile([P, TOP, T], F32, name="gates", align_bytes=64)
-        by_column = gates[:].rearrange("p r (h i n) -> p i (r h) n", h=2, n=16)
-        for b in range(4):
-            spread = psum.tile([P, 4, P // 16, 16], F32, name="spread", tag="bank")
-            for i in range(4):
-                column = gate_columns[:, 4 * b + i : 4 * b + i + 1].to_broadcast([P, P])
-                nc.tensor.transpose(spread[:, i].rearrange("p q n -> p (q n)"), column, identity[:])
-            nc.scalar.copy(by_column[:, 4 * b : 4 * (b + 1)], spread[:, :, : 2 * TOP, :])
+        for r in range(TOP):
+            spread = psum.tile([P, T], F32, name="spread", tag="bank")
+            for i in range(T // P):
+                column = gate_columns[:, r, i : i + 1].to_broadcast([P, P])
+                nc.tensor.transpose(spread[:, i * P : (i + 1) * P], column, identity[:])
+            nc.scalar.copy(gates[:, r, :], spread[:])
 
         def gather(table, dtype, name):
             picked = keep.tile([P, E * C], dtype, name=name, align_bytes=64)
@@ -136,10 +132,13 @@ def tile_moe_tk_mlp_relu_kernel(tc, xT, w1, w2, gate, offs, pos1, pos2, pos3, ou
 
         def quantise_chunk(raw, e, s, share, step):
             grouped = groups.tile([P, H, J], BF16, name="w1_grouped", tag="grouped", align_bytes=64)
-            shared_copy(
-                grouped[:].rearrange("p (t m) j -> p m j t", t=HT), raw.rearrange("p j (m t) -> p m j t", t=HT), share,
-                e < E - 1,
-            )
+            dst = grouped[:].rearrange("p (t m) j -> p m j t", t=HT)
+            src = raw.rearrange("p j (m t) -> p m j t", t=HT)
+            if step < H:
+                nc.vector.tensor_copy(out=dst[:, :, :, :2], in_=src[:, :, :, :2])
+                nc.scalar.activation(dst[:, :, :, 2:], src[:, :, :, 2:], COPY)
+            else:
+                shared_copy(dst, src, share, e < E - 1)
             words = codes.tile([P, H], U32, name="w1_words", align_bytes=64)
             scales = codes.tile([P, H], U8, name="w1_scales", align_bytes=64)
             for lo in range(0, H, step):
@@ -245,7 +244,8 @@ def tile_moe_tk_mlp_relu_kernel(tc, xT, w1, w2, gate, offs, pos1, pos2, pos3, ou
         for e in range(E):
             words = keep.tile([P, N], U32, name=f"w2_words{e}", align_bytes=64)
             scales = keep.tile([P, N], U8, name=f"w2_scales{e}", align_bytes=64)
-            quantise(words[:], scales[:], w2_grouped[e][:].rearrange("p n j -> p (n j)"))
+            for lo, hi in ((N // 2, N), (0, N // 2)) if e == E - 1 else ((0, N),):
+                quantise(words[:, lo:hi], scales[:, lo:hi], w2_grouped[e][:, lo:hi, :].rearrange("p n j -> p (n j)"))
             w2_codes.append((words, scales))
 
 
@@ -294,7 +294,6 @@ def tile_moe_tk_mlp_relu_kernel(tc, xT, w1, w2, gate, offs, pos1, pos2, pos3, ou
             nc.tensor.transpose(back[:], rows, identity[:])
             sums.append(back)
         nc.scalar.copy(total[:, tiles[0]], sums[0][:])
-        nc.sync.dma_start(out=out[:, tiles[0]], in_=total[:, tiles[0]])
 
         gather_times_gate(products[2], 2, tiles[1])
         for r in range(TOP):
@@ -303,7 +302,7 @@ def tile_moe_tk_mlp_relu_kernel(tc, xT, w1, w2, gate, offs, pos1, pos2, pos3, ou
         nc.vector.tensor_tensor(last_pair[:], products[0][:, tiles[3]], products[1][:, tiles[3]], ADD)
         gather_times_gate(products[2], 2, tiles[2])
         nc.vector.tensor_tensor(total[:, tiles[1]], products[2][:, tiles[1]], sums[1][:], ADD)
-        nc.sync.dma_start(out=out[:, tiles[1]], in_=total[:, tiles[1]])
+        nc.sync.dma_start(out=out[:, : T // 2], in_=total[:, : T // 2])
         nc.vector.tensor_tensor(total[:, tiles[3]], products[2][:, tiles[3]], last_pair[:], ADD)
         nc.vector.tensor_tensor(total[:, tiles[2]], products[2][:, tiles[2]], sums[2][:], ADD)
         nc.sync.dma_start(out=out[:, T // 2 :], in_=total[:, T // 2 :])

@@ -25,22 +25,16 @@ M = P
 HT = H // M
 HALF = C // 2
 HALVES = ((0, HALF), (HALF, C))
-LIST = C // 16
 SCALE_ROWS = 4
-
-X_SHARE = 16
-SHARE_WHILE_GATHERING = 40
-SHARE_CATCHING_UP = 56
-SHARE_LAST = 84
 GATHER = 384
-VECTOR_FROM = 7
-GATHER_AHEAD = 2
-GATHER_WORDS_AT = 1
-GATHER_SCALES_AT = 3
-HIDDEN_AT = 2
-PASS_BY_PASS = 2
+
+VECTOR_CHUNK = 7
+SHARED_FROM = 2
+SHARE_CATCHING_UP = 56
+CAUGHT_UP = 4
+HIDDEN_AT_EARLY = 2
 W2_ON_VECTOR = (0, 3, 4)
-W2_LAST_SHARE = 16
+Y_ON_VECTOR = (3, 4, 6)
 
 DMA_ALIGN = 256
 STAGE_BUFS = 11
@@ -62,14 +56,11 @@ def tile_moe_tk_mlp_relu_kernel(tc, xT, w1, w2, gate, offs, pos1, pos2, pos3, ou
             nc.sync.dma_start(out=raw[:], in_=rows.rearrange("(p j) c -> p j c", j=J))
             return raw[:]
 
-        def shared_copy(dst, src, share, halved=False):
+        def shared_copy(dst, src, share):
             if share > 0:
                 nc.vector.tensor_copy(out=dst[:, :share], in_=src[:, :share])
             if share < dst.shape[1]:
-                middle = (share + dst.shape[1]) // 2 if halved else dst.shape[1]
-                nc.scalar.activation(dst[:, share:middle], src[:, share:middle], COPY)
-                if halved:
-                    nc.scalar.activation(dst[:, middle:], src[:, middle:], COPY)
+                nc.scalar.activation(dst[:, share:], src[:, share:], COPY)
 
         def interleaved(rows, grouped):
             return grouped.rearrange("p (c i) j -> p c j i", i=4), rows.rearrange("p j (c i) -> p c j i", i=4)
@@ -99,7 +90,7 @@ def tile_moe_tk_mlp_relu_kernel(tc, xT, w1, w2, gate, offs, pos1, pos2, pos3, ou
                 nc.sync.dma_start(offsets[:], offs)
             raw = load_pass(xT[s * P * J : (s + 1) * P * J, :], stage, "raw")
             grouped = groups.tile([P, T, J], BF16, name="x_grouped", tag="grouped", align_bytes=64)
-            shared_copy(*interleaved(raw, grouped[:]), M if s == 0 else 0, True)
+            shared_copy(*interleaved(raw, grouped[:]), T // 4 if s == 0 else 0)
             words = keep.tile([P, T], U32, name=f"x_words{s}", align_bytes=64)
             quantise(words[:], x_scales[SCALE_ROWS * s :, :], grouped[:].rearrange("p t j -> p (t j)"))
             x_words.append(words)
@@ -130,17 +121,18 @@ def tile_moe_tk_mlp_relu_kernel(tc, xT, w1, w2, gate, offs, pos1, pos2, pos3, ou
         slot_words = [gather(x_words[s], U32, f"slot_words{s}") for s in range(S)]
         slot_scales = gather(x_scales, U8, "slot_scales")
 
-        def quantise_chunk(raw, e, s, share, step):
+        def quantise_chunk(raw, share, by_tiles):
             grouped = groups.tile([P, H, J], BF16, name="w1_grouped", tag="grouped", align_bytes=64)
             dst = grouped[:].rearrange("p (t m) j -> p m j t", t=HT)
             src = raw.rearrange("p j (m t) -> p m j t", t=HT)
-            if step < H:
-                nc.vector.tensor_copy(out=dst[:, :, :, :2], in_=src[:, :, :, :2])
-                nc.scalar.activation(dst[:, :, :, 2:], src[:, :, :, 2:], COPY)
+            if by_tiles:
+                nc.vector.tensor_copy(out=dst[:, :, :, : HT // 2], in_=src[:, :, :, : HT // 2])
+                nc.scalar.activation(dst[:, :, :, HT // 2 :], src[:, :, :, HT // 2 :], COPY)
             else:
-                shared_copy(dst, src, share, e < E - 1)
+                shared_copy(dst, src, share)
             words = codes.tile([P, H], U32, name="w1_words", align_bytes=64)
             scales = codes.tile([P, H], U8, name="w1_scales", align_bytes=64)
+            step = M if by_tiles else H
             for lo in range(0, H, step):
                 values = grouped[:, lo : lo + step, :].rearrange("p h j -> p (h j)")
                 quantise(words[:, lo : lo + step], scales[:, lo : lo + step], values)
@@ -154,12 +146,12 @@ def tile_moe_tk_mlp_relu_kernel(tc, xT, w1, w2, gate, offs, pos1, pos2, pos3, ou
                 opens and s == 0, closes and s == S - 1,
             )
 
-        def quantise_hidden(e, halves):
+        def quantise_hidden(e, parts):
             words = keep.tile([P, C], U32, name=f"h_words{e}", align_bytes=64)
             scales = keep.tile([P, C], U8, name=f"h_scales{e}", align_bytes=64)
-            step = C // len(halves)
-            for i, half in enumerate(halves):
-                quantise(words[:, i * step : (i + 1) * step], scales[:, i * step : (i + 1) * step], half)
+            step = C // len(parts)
+            for i, part in enumerate(parts):
+                quantise(words[:, i * step : (i + 1) * step], scales[:, i * step : (i + 1) * step], part)
             hidden.append((words, scales))
 
         def rows_out(rows, banks):
@@ -180,26 +172,27 @@ def tile_moe_tk_mlp_relu_kernel(tc, xT, w1, w2, gate, offs, pos1, pos2, pos3, ou
             chunks = []
             if last:
                 tile_banks = [psum.tile([P, HT, HALF], F32, name="h_bank", tag="bank") for half in HALVES]
-            elif e >= PASS_BY_PASS:
+            elif e >= SHARED_FROM:
                 tile_banks = [psum.tile([P, C], F32, name="tile_bank", tag="bank") for t in range(HT)]
             for s in range(S):
                 raw = load_pass(w1[e, s * P * J : (s + 1) * P * J, :], stage, "raw")
-                share = M if s % 2 == 1 and e * S + s >= VECTOR_FROM else 0
-                if e >= PASS_BY_PASS:
-                    share = SHARE_LAST if last and s == S - 1 else M // 2 if e >= E - 2 else SHARE_CATCHING_UP
-                chunks.append(quantise_chunk(raw, e, s, share, M if last and s == S - 1 else H))
+                if e < SHARED_FROM:
+                    share = M if e * S + s == VECTOR_CHUNK else 0
+                else:
+                    share = SHARE_CATCHING_UP if e < CAUGHT_UP else M // 2
+                chunks.append(quantise_chunk(raw, share, last and s == S - 1))
                 if last:
-                    for bank, (lo, hi), tiles in zip(tile_banks, HALVES, (range(HT), reversed(range(HT)))):
-                        for i, t in enumerate(tiles):
+                    for bank, (lo, hi), order in zip(tile_banks, HALVES, (range(HT), reversed(range(HT)))):
+                        for i, t in enumerate(order):
                             first_product(bank[:, t, :], chunks[s], t, e, s, lo, hi, i == 0, i == HT - 1)
-                elif e >= PASS_BY_PASS:
+                elif e >= SHARED_FROM:
                     for t in range(HT):
                         first_product(tile_banks[t][:], chunks[s], t, e, s, 0, C)
-                if s == 0 and e > PASS_BY_PASS:
+                if s == 0 and e > SHARED_FROM:
                     rows = raw[:, :, H - C // 2 :].bitcast(BF16)
                     rows_out(rows, h_banks)
                     interleave_hidden(e - 1, rows)
-                if s == HIDDEN_AT and 0 < e <= PASS_BY_PASS:
+                if s == HIDDEN_AT_EARLY and 0 < e <= SHARED_FROM:
                     values = raw[:, J - 1, :].bitcast(BF16)
                     for (lo, hi), bank in zip(HALVES, h_banks):
                         nc.scalar.activation(
@@ -208,7 +201,7 @@ def tile_moe_tk_mlp_relu_kernel(tc, xT, w1, w2, gate, offs, pos1, pos2, pos3, ou
                             RELU,
                         )
                     quantise_hidden(e - 1, [values])
-            if e >= PASS_BY_PASS:
+            if e >= SHARED_FROM:
                 h_banks = tile_banks
             else:
                 h_banks = []
@@ -231,7 +224,7 @@ def tile_moe_tk_mlp_relu_kernel(tc, xT, w1, w2, gate, offs, pos1, pos2, pos3, ou
             grouped = keep.tile([P, N, J], BF16, name=f"w2_grouped{e}", align_bytes=64)
             dst, src = interleaved(w2_raw[e], grouped[:])
             if e == E - 1:
-                shared_copy(dst, src, W2_LAST_SHARE)
+                shared_copy(dst, src, dst.shape[1] // 2)
             elif e in W2_ON_VECTOR:
                 nc.vector.tensor_copy(out=dst, in_=src)
             else:
@@ -248,7 +241,6 @@ def tile_moe_tk_mlp_relu_kernel(tc, xT, w1, w2, gate, offs, pos1, pos2, pos3, ou
                 quantise(words[:, lo:hi], scales[:, lo:hi], w2_grouped[e][:, lo:hi, :].rearrange("p n j -> p (n j)"))
             w2_codes.append((words, scales))
 
-
         pieces = [(e, 0, C) for e in range(E - 1)] + [(E - 1, lo, hi) for lo, hi in HALVES]
         for i, (e, lo, hi) in enumerate(pieces):
             acc = psum.tile([P, C], F32, name="y_bank", tag="bank")
@@ -256,7 +248,7 @@ def tile_moe_tk_mlp_relu_kernel(tc, xT, w1, w2, gate, offs, pos1, pos2, pos3, ou
                 acc[:, : hi - lo], w2_codes[e][0][:], w2_codes[e][1][:], hidden[e][0][:, lo:hi], hidden[e][1][:, lo:hi],
                 True, True,
             )
-            copy_out = nc.vector.tensor_copy if i in (0, 4, 6) else nc.scalar.copy
+            copy_out = nc.vector.tensor_copy if i in Y_ON_VECTOR else nc.scalar.copy
             copy_out(y[:, e * C + lo : e * C + hi], acc[:, : hi - lo])
 
         places = [keep.tile([P, T // 16], U16, name=f"place{r}") for r in range(TOP)]
@@ -264,45 +256,48 @@ def tile_moe_tk_mlp_relu_kernel(tc, xT, w1, w2, gate, offs, pos1, pos2, pos3, ou
             nc.sync.dma_start(places[r][:], pos)
 
         products = [keep.tile([P, T], F32, name=f"scaled{r}", align_bytes=64) for r in range(TOP)]
-
-        def gather_times_gate(product, r, cols):
-            where = places[r][:, cols.start // 16 : cols.stop // 16]
-            nc.vector.tensor_tensor(product[:, cols], y[:].indirect(where), gates[:, r, cols], MULT)
-
-        tiles = [slice(lo, lo + P) for lo in range(0, T, P)]
+        token_tiles = [slice(lo, lo + P) for lo in range(0, T, P)]
         total = keep.tile([P, T], F32, name="total", align_bytes=DMA_ALIGN)
-        turned = [psum.tile([P, P], F32, name="turned", tag="bank") for i in range(3)]
+        turned = [psum.tile([P, P], F32, name="turned", tag="bank") for cols in token_tiles[:-1]]
+
+        def gather_times_gate(r, cols):
+            where = places[r][:, cols.start // 16 : cols.stop // 16]
+            nc.vector.tensor_tensor(products[r][:, cols], y[:].indirect(where), gates[:, r, cols], MULT)
 
         def turn(r, i, stop):
-            nc.tensor.matmul(turned[i][:], products[r][:, tiles[i]], identity[:], start=r == 0, stop=stop, is_transpose=True)
+            product = products[r][:, token_tiles[i]]
+            nc.tensor.matmul(turned[i][:], product, identity[:], start=r == 0, stop=stop, is_transpose=True)
 
-        gather_times_gate(products[0], 0, slice(0, 3 * P))
-        for i in range(3):
+        def add_third(i, pair):
+            cols = token_tiles[i]
+            nc.vector.tensor_tensor(total[:, cols], products[2][:, cols], pair, ADD)
+
+        gather_times_gate(0, slice(0, len(turned) * P))
+        for i in range(len(turned)):
             turn(0, i, False)
-        gather_times_gate(products[1], 1, tiles[0])
-        turn(1, 0, False)
-        gather_times_gate(products[2], 2, tiles[0])
-        turn(2, 0, True)
+        for r in (1, 2):
+            gather_times_gate(r, token_tiles[0])
+            turn(r, 0, r == 2)
         for i in (1, 2):
-            gather_times_gate(products[1], 1, tiles[i])
+            gather_times_gate(1, token_tiles[i])
             turn(1, i, True)
         summed = keep.tile([P, 2, P], F32, name="summed", align_bytes=64)
         sums = []
-        for bank, rows in zip(turned, (summed[:, 0, :], total[:, tiles[3]], summed[:, 1, :])):
+        for bank, rows in zip(turned, (summed[:, 0, :], total[:, token_tiles[3]], summed[:, 1, :])):
             nc.scalar.copy(rows, bank[:])
             back = psum.tile([P, P], F32, name="back", tag="bank")
             nc.tensor.transpose(back[:], rows, identity[:])
             sums.append(back)
-        nc.scalar.copy(total[:, tiles[0]], sums[0][:])
+        nc.scalar.copy(total[:, token_tiles[0]], sums[0][:])
 
-        gather_times_gate(products[2], 2, tiles[1])
+        gather_times_gate(2, token_tiles[1])
         for r in range(TOP):
-            gather_times_gate(products[r], r, tiles[3])
+            gather_times_gate(r, token_tiles[3])
         last_pair = keep.tile([P, P], F32, name="last_pair", align_bytes=64)
-        nc.vector.tensor_tensor(last_pair[:], products[0][:, tiles[3]], products[1][:, tiles[3]], ADD)
-        gather_times_gate(products[2], 2, tiles[2])
-        nc.vector.tensor_tensor(total[:, tiles[1]], products[2][:, tiles[1]], sums[1][:], ADD)
+        nc.vector.tensor_tensor(last_pair[:], products[0][:, token_tiles[3]], products[1][:, token_tiles[3]], ADD)
+        gather_times_gate(2, token_tiles[2])
+        add_third(1, sums[1][:])
         nc.sync.dma_start(out=out[:, : T // 2], in_=total[:, : T // 2])
-        nc.vector.tensor_tensor(total[:, tiles[3]], products[2][:, tiles[3]], last_pair[:], ADD)
-        nc.vector.tensor_tensor(total[:, tiles[2]], products[2][:, tiles[2]], sums[2][:], ADD)
+        add_third(3, last_pair[:])
+        add_third(2, sums[2][:])
         nc.sync.dma_start(out=out[:, T // 2 :], in_=total[:, T // 2 :])

@@ -26,7 +26,7 @@ HT = H // M
 HALF = C // 2
 HALVES = ((0, HALF), (HALF, C))
 SCALE_ROWS = 4
-GATHER = 384
+WINDOW = 2048
 
 VECTOR_CHUNK = 7
 SHARED_FROM = 2
@@ -79,21 +79,21 @@ def tile_moe_tk_mlp_relu_kernel(tc, xT, w1, w2, gate, offs, pos1, pos2, pos3, ou
                 stop=stop,
             )
 
-        x_scales = keep.tile([P, T], U8, name="x_scales", align_bytes=64)
-        nc.gpsimd.memset(x_scales[:], 0)
+        x_scales = keep.tile([P, WINDOW], U8, name="x_scales", align_bytes=64)
+        nc.gpsimd.memset(x_scales[:].bitcast(U32), 0)
+        x_words = keep.tile([P, (S - 1) * T + WINDOW], U32, name="x_words", align_bytes=64)
+        nc.gpsimd.memset(x_words[:, S * T :], 0)
         identity = keep.tile([P, P], F32, name="identity", align_bytes=64)
         make_identity(nc, identity[:])
         offsets = keep.tile([P, TOP * T // 16], U16, name="offsets")
-        x_words = []
         for s in range(S):
             if s == S // 2:
                 nc.sync.dma_start(offsets[:], offs)
             raw = load_pass(xT[s * P * J : (s + 1) * P * J, :], stage, "raw")
             grouped = groups.tile([P, T, J], BF16, name="x_grouped", tag="grouped", align_bytes=64)
             shared_copy(*interleaved(raw, grouped[:]), T // 4 if s == 0 else 0)
-            words = keep.tile([P, T], U32, name=f"x_words{s}", align_bytes=64)
-            quantise(words[:], x_scales[SCALE_ROWS * s :, :], grouped[:].rearrange("p t j -> p (t j)"))
-            x_words.append(words)
+            first = (S - 1 - s) * T
+            quantise(x_words[:, first : first + T], x_scales[SCALE_ROWS * s :, :T], grouped[:].rearrange("p t j -> p (t j)"))
 
         gate_rows = keep.tile([P, TOP, P], F32, name="gate_rows", align_bytes=DMA_ALIGN)
         nc.gpsimd.memset(gate_rows[:], 0.0)
@@ -113,13 +113,11 @@ def tile_moe_tk_mlp_relu_kernel(tc, xT, w1, w2, gate, offs, pos1, pos2, pos3, ou
 
         def gather(table, dtype, name):
             picked = keep.tile([P, E * C], dtype, name=name, align_bytes=64)
-            for lo in range(0, E * C, GATHER):
-                where = offsets[:, lo // 16 : (lo + GATHER) // 16]
-                nc.vector.tensor_copy(picked[:, lo : lo + GATHER], table[:].indirect(where))
+            nc.vector.tensor_copy(picked[:], table.indirect(offsets[:]))
             return picked
 
-        slot_words = [gather(x_words[s], U32, f"slot_words{s}") for s in range(S)]
-        slot_scales = gather(x_scales, U8, "slot_scales")
+        slot_words = [gather(x_words[:, (S - 1 - s) * T :][:, :WINDOW], U32, f"slot_words{s}") for s in range(S)]
+        slot_scales = gather(x_scales[:], U8, "slot_scales")
 
         def quantise_chunk(raw, share, by_tiles):
             grouped = groups.tile([P, H, J], BF16, name="w1_grouped", tag="grouped", align_bytes=64)
@@ -160,10 +158,9 @@ def tile_moe_tk_mlp_relu_kernel(tc, xT, w1, w2, gate, offs, pos1, pos2, pos3, ou
 
         def interleave_hidden(e, rows):
             grouped = keep.tile([P, C, HT], BF16, name=f"h_grouped{e}", align_bytes=64)
-            for lo, hi in HALVES:
-                dst, src = interleaved(rows[:, :, lo:hi], grouped[:, lo:hi, :])
-                nc.vector.tensor_copy(out=dst, in_=src)
-            quantise_hidden(e, [grouped[:, lo:hi, :].rearrange("p c t -> p (c t)") for lo, hi in HALVES])
+            dst, src = interleaved(rows, grouped[:])
+            nc.vector.tensor_copy(out=dst, in_=src)
+            quantise_hidden(e, [grouped[:].rearrange("p c t -> p (c t)")])
 
         hidden = []
         h_banks = []

@@ -27,19 +27,17 @@ HALF = C // 2
 HALVES = ((0, HALF), (HALF, C))
 SCALE_ROWS = 4
 WINDOW = 2048
-
-VECTOR_CHUNK = 7
-SHARED_FROM = 2
-SHARE_CATCHING_UP = 56
-CAUGHT_UP = 4
-HIDDEN_AT_EARLY = 2
-W2_ON_VECTOR = (0, 3, 4)
-Y_ON_VECTOR = (3, 4, 6)
-
 DMA_ALIGN = 256
 STAGE_BUFS = 11
 GROUPED_BUFS = 8
 CODE_BUFS = 2 * S
+HIDDEN_AT = 1
+VECTOR_CHUNK = 7
+SHARED_FROM = 2
+SHARE_CATCHING_UP = 56
+CAUGHT_UP = 4
+W2_ON_VECTOR = (0, 3, 4)
+Y_ON_VECTOR = (3, 4, 6)
 
 
 def tile_moe_tk_mlp_relu_kernel(tc, xT, w1, w2, gate, offs, pos1, pos2, pos3, out):
@@ -95,18 +93,20 @@ def tile_moe_tk_mlp_relu_kernel(tc, xT, w1, w2, gate, offs, pos1, pos2, pos3, ou
             first = (S - 1 - s) * T
             quantise(x_words[:, first : first + T], x_scales[SCALE_ROWS * s :, :T], grouped[:].rearrange("p t j -> p (t j)"))
 
+        tiles = T // P
+        turned_tile = tiles - 1
         gate_rows = keep.tile([P, TOP, P], F32, name="gate_rows", align_bytes=DMA_ALIGN)
         nc.gpsimd.memset(gate_rows[:], 0.0)
-        nc.sync.dma_start(out=gate_rows[: T // P], in_=gate[:, 0, :].rearrange("r (i n) -> i r n", n=P))
+        nc.sync.dma_start(out=gate_rows[:tiles], in_=gate[:, 0, :].rearrange("r (i n) -> i r n", n=P))
         turned_rows = psum.tile([P, TOP, P], F32, name="turned_rows", tag="bank")
         for r in range(TOP):
             nc.tensor.transpose(turned_rows[:, r, :], gate_rows[:, r, :], identity[:])
-        gate_columns = keep.tile([P, TOP, T // P], F32, name="gate_columns", align_bytes=64)
-        nc.scalar.copy(gate_columns[:], turned_rows[:, :, : T // P])
-        gates = keep.tile([P, TOP, T], F32, name="gates", align_bytes=64)
+        gate_columns = keep.tile([P, TOP, tiles], F32, name="gate_columns", align_bytes=64)
+        nc.scalar.copy(gate_columns[:], turned_rows[:, :, :tiles])
+        gates = keep.tile([P, TOP, turned_tile * P], F32, name="gates", align_bytes=64)
         for r in range(TOP):
-            spread = psum.tile([P, T], F32, name="spread", tag="bank")
-            for i in range(T // P):
+            spread = psum.tile([P, turned_tile * P], F32, name="spread", tag="bank")
+            for i in range(turned_tile):
                 column = gate_columns[:, r, i : i + 1].to_broadcast([P, P])
                 nc.tensor.transpose(spread[:, i * P : (i + 1) * P], column, identity[:])
             nc.scalar.copy(gates[:, r, :], spread[:])
@@ -136,13 +136,8 @@ def tile_moe_tk_mlp_relu_kernel(tc, xT, w1, w2, gate, offs, pos1, pos2, pos3, ou
                 quantise(words[:, lo : lo + step], scales[:, lo : lo + step], values)
             return words, scales
 
-        def first_product(acc, chunk, t, e, s, lo, hi, opens=True, closes=True):
-            cols = slice(t * M, (t + 1) * M)
-            slots = slice(e * C + lo, e * C + hi)
-            matmul(
-                acc, chunk[0][:, cols], chunk[1][:, cols], slot_words[s][:, slots], slot_scales[SCALE_ROWS * s :, slots],
-                opens and s == 0, closes and s == S - 1,
-            )
+        def relu_out(values, bank):
+            nc.scalar.activation(values.rearrange("p (c t) -> p c t", t=HT), bank[:].rearrange("p t c -> p c t"), RELU)
 
         def quantise_hidden(e, parts):
             words = keep.tile([P, C], U32, name=f"h_words{e}", align_bytes=64)
@@ -152,69 +147,38 @@ def tile_moe_tk_mlp_relu_kernel(tc, xT, w1, w2, gate, offs, pos1, pos2, pos3, ou
                 quantise(words[:, i * step : (i + 1) * step], scales[:, i * step : (i + 1) * step], part)
             hidden.append((words, scales))
 
-        def rows_out(rows, banks):
-            for t in range(HT):
-                nc.scalar.activation(rows[:, t, :], banks[t][:], RELU)
-
-        def interleave_hidden(e, rows):
-            grouped = keep.tile([P, C, HT], BF16, name=f"h_grouped{e}", align_bytes=64)
-            dst, src = interleaved(rows, grouped[:])
-            nc.vector.tensor_copy(out=dst, in_=src)
-            quantise_hidden(e, [grouped[:].rearrange("p c t -> p (c t)")])
-
         hidden = []
         h_banks = []
         for e in range(E):
-            last = e == E - 1
-            chunks = []
-            if last:
-                tile_banks = [psum.tile([P, HT, HALF], F32, name="h_bank", tag="bank") for half in HALVES]
-            elif e >= SHARED_FROM:
-                tile_banks = [psum.tile([P, C], F32, name="tile_bank", tag="bank") for t in range(HT)]
+            banks = [psum.tile([P, HT, HALF], F32, name="h_bank", tag="bank") for half in HALVES]
             for s in range(S):
                 raw = load_pass(w1[e, s * P * J : (s + 1) * P * J, :], stage, "raw")
                 if e < SHARED_FROM:
                     share = M if e * S + s == VECTOR_CHUNK else 0
                 else:
                     share = SHARE_CATCHING_UP if e < CAUGHT_UP else M // 2
-                chunks.append(quantise_chunk(raw, share, last and s == S - 1))
-                if last:
-                    for bank, (lo, hi), order in zip(tile_banks, HALVES, (range(HT), reversed(range(HT)))):
-                        for i, t in enumerate(order):
-                            first_product(bank[:, t, :], chunks[s], t, e, s, lo, hi, i == 0, i == HT - 1)
-                elif e >= SHARED_FROM:
-                    for t in range(HT):
-                        first_product(tile_banks[t][:], chunks[s], t, e, s, 0, C)
-                if s == 0 and e > SHARED_FROM:
-                    rows = raw[:, :, H - C // 2 :].bitcast(BF16)
-                    rows_out(rows, h_banks)
-                    interleave_hidden(e - 1, rows)
-                if s == HIDDEN_AT_EARLY and 0 < e <= SHARED_FROM:
+                words, scales = quantise_chunk(raw, share, e == E - 1 and s == S - 1)
+                for bank, (lo, hi), order in zip(banks, HALVES, (range(HT), reversed(range(HT)))):
+                    slots = slice(e * C + lo, e * C + hi)
+                    for i, t in enumerate(order):
+                        cols = slice(t * M, (t + 1) * M)
+                        matmul(
+                            bank[:, t, :], words[:, cols], scales[:, cols], slot_words[s][:, slots],
+                            slot_scales[SCALE_ROWS * s :, slots], s == 0 and i == 0, s == S - 1 and i == HT - 1,
+                        )
+                if s == HIDDEN_AT and e > 0:
                     values = raw[:, J - 1, :].bitcast(BF16)
                     for (lo, hi), bank in zip(HALVES, h_banks):
-                        nc.scalar.activation(
-                            values[:, lo * HT : hi * HT].rearrange("p (c t) -> p c t", t=HT),
-                            bank[:].rearrange("p t c -> p c t"),
-                            RELU,
-                        )
+                        relu_out(values[:, lo * HT : hi * HT], bank)
                     quantise_hidden(e - 1, [values])
-            if e >= SHARED_FROM:
-                h_banks = tile_banks
-            else:
-                h_banks = []
-                for lo, hi in HALVES:
-                    bank = psum.tile([P, HT, HALF], F32, name="h_bank", tag="bank")
-                    for t in range(HT):
-                        for s in range(S):
-                            first_product(bank[:, t, :], chunks[s], t, e, s, lo, hi)
-                    h_banks.append(bank)
+            h_banks = banks
 
         w2_raw = [load_pass(w2[e], *((keep, "y") if e == E - 1 else (stage, "raw"))) for e in range(E)]
         y = keep.tile([P, E * C], F32, name="y", tag="y", align_bytes=DMA_ALIGN)
 
-        h_last = [keep.tile([P, HALF, HT], BF16, name=f"h_last{lo}", align_bytes=64) for lo, hi in HALVES]
+        h_last = [keep.tile([P, HALF * HT], BF16, name=f"h_last{lo}", align_bytes=64) for lo, hi in HALVES]
         for half, bank in zip(h_last, h_banks):
-            nc.scalar.activation(half[:], bank[:].rearrange("p t c -> p c t"), RELU)
+            relu_out(half[:], bank)
 
         w2_grouped = []
         for e in range(E):
@@ -228,7 +192,7 @@ def tile_moe_tk_mlp_relu_kernel(tc, xT, w1, w2, gate, offs, pos1, pos2, pos3, ou
                 nc.scalar.activation(dst, src, COPY)
             w2_grouped.append(grouped)
 
-        quantise_hidden(E - 1, [half[:].rearrange("p c t -> p (c t)") for half in h_last])
+        quantise_hidden(E - 1, [half[:] for half in h_last])
 
         w2_codes = []
         for e in range(E):
@@ -252,49 +216,37 @@ def tile_moe_tk_mlp_relu_kernel(tc, xT, w1, w2, gate, offs, pos1, pos2, pos3, ou
         for r, pos in enumerate((pos1, pos2, pos3)):
             nc.sync.dma_start(places[r][:], pos)
 
-        products = [keep.tile([P, T], F32, name=f"scaled{r}", align_bytes=64) for r in range(TOP)]
-        token_tiles = [slice(lo, lo + P) for lo in range(0, T, P)]
+        def picked(r, cols):
+            return y[:].indirect(places[r][:, cols.start // 16 : cols.stop // 16])
+
         total = keep.tile([P, T], F32, name="total", align_bytes=DMA_ALIGN)
-        turned = [psum.tile([P, P], F32, name="turned", tag="bank") for cols in token_tiles[:-1]]
+        early, late, direct, turned = slice(0, 2 * P), slice(2 * P, 3 * P), slice(0, 3 * P), slice(3 * P, T)
 
-        def gather_times_gate(r, cols):
-            where = places[r][:, cols.start // 16 : cols.stop // 16]
-            nc.vector.tensor_tensor(products[r][:, cols], y[:].indirect(where), gates[:, r, cols], MULT)
-
-        def turn(r, i, stop):
-            product = products[r][:, token_tiles[i]]
-            nc.tensor.matmul(turned[i][:], product, identity[:], start=r == 0, stop=stop, is_transpose=True)
-
-        def add_third(i, pair):
-            cols = token_tiles[i]
-            nc.vector.tensor_tensor(total[:, cols], products[2][:, cols], pair, ADD)
-
-        gather_times_gate(0, slice(0, len(turned) * P))
-        for i in range(len(turned)):
-            turn(0, i, False)
-        for r in (1, 2):
-            gather_times_gate(r, token_tiles[0])
-            turn(r, 0, r == 2)
-        for i in (1, 2):
-            gather_times_gate(1, token_tiles[i])
-            turn(1, i, True)
-        summed = keep.tile([P, 2, P], F32, name="summed", align_bytes=64)
-        sums = []
-        for bank, rows in zip(turned, (summed[:, 0, :], total[:, token_tiles[3]], summed[:, 1, :])):
-            nc.scalar.copy(rows, bank[:])
-            back = psum.tile([P, P], F32, name="back", tag="bank")
-            nc.tensor.transpose(back[:], rows, identity[:])
-            sums.append(back)
-        nc.scalar.copy(total[:, token_tiles[0]], sums[0][:])
-
-        gather_times_gate(2, token_tiles[1])
+        turned_banks = []
         for r in range(TOP):
-            gather_times_gate(r, token_tiles[3])
-        last_pair = keep.tile([P, P], F32, name="last_pair", align_bytes=64)
-        nc.vector.tensor_tensor(last_pair[:], products[0][:, token_tiles[3]], products[1][:, token_tiles[3]], ADD)
-        gather_times_gate(2, token_tiles[2])
-        add_third(1, sums[1][:])
+            plain = keep.tile([P, P], F32, name=f"plain{r}", align_bytes=64)
+            nc.scalar.activation(plain[:], picked(r, turned), COPY)
+            bank = psum.tile([P, P], F32, name="turned", tag="bank")
+            nc.tensor.transpose(bank[:], plain[:], identity[:])
+            turned_banks.append(bank)
+        firsts = keep.tile([P, 3 * P], F32, name="firsts", align_bytes=64)
+        nc.scalar.activation(firsts[:, early], picked(0, early), COPY)
+        back = psum.tile([P, P], F32, name="back", tag="bank")
+        for r in range(TOP):
+            scaled = keep.tile([P, P], F32, name=f"scaled{r}", align_bytes=64)
+            nc.scalar.activation(scaled[:], turned_banks[r][:], COPY, scale=gate_columns[:, r, turned_tile : turned_tile + 1])
+            nc.tensor.matmul(back[:], scaled[:], identity[:], start=r == 0, stop=r == TOP - 1, is_transpose=True)
+        nc.scalar.activation(firsts[:, late], picked(0, late), COPY)
+        nc.scalar.copy(total[:, turned], back[:])
+
+        products = [keep.tile([P, 3 * P], F32, name=f"product{r}", align_bytes=64) for r in range(TOP)]
+        pair = keep.tile([P, 3 * P], F32, name="pair", align_bytes=64)
+        for r in (2, 1):
+            nc.vector.tensor_tensor(products[r][:], picked(r, direct), gates[:, r, :], MULT)
+        nc.vector.tensor_tensor(products[0][:, early], firsts[:, early], gates[:, 0, early], MULT)
+        nc.vector.tensor_tensor(pair[:], products[1][:], products[2][:], ADD)
+        nc.vector.tensor_tensor(products[0][:, late], firsts[:, late], gates[:, 0, late], MULT)
+        nc.vector.tensor_tensor(total[:, early], pair[:, early], products[0][:, early], ADD)
         nc.sync.dma_start(out=out[:, : T // 2], in_=total[:, : T // 2])
-        add_third(3, last_pair[:])
-        add_third(2, sums[2][:])
+        nc.vector.tensor_tensor(total[:, late], pair[:, late], products[0][:, late], ADD)
         nc.sync.dma_start(out=out[:, T // 2 :], in_=total[:, T // 2 :])

@@ -32,6 +32,7 @@ STAGE_BUFS = 11
 GROUPED_BUFS = 8
 CODE_BUFS = 2 * S
 HIDDEN_AT = 1
+SCALAR_PIECES = 4
 VECTOR_CHUNK = 7
 SHARED_FROM = 2
 SHARE_CATCHING_UP = 56
@@ -57,8 +58,10 @@ def tile_moe_tk_mlp_relu_kernel(tc, xT, w1, w2, gate, offs, pos1, pos2, pos3, ou
         def shared_copy(dst, src, share):
             if share > 0:
                 nc.vector.tensor_copy(out=dst[:, :share], in_=src[:, :share])
-            if share < dst.shape[1]:
-                nc.scalar.activation(dst[:, share:], src[:, share:], COPY)
+            pieces = SCALAR_PIECES if share == 0 else 1
+            step = (dst.shape[1] - share) // pieces
+            for lo in range(share, dst.shape[1], max(step, 1)):
+                nc.scalar.activation(dst[:, lo : lo + step], src[:, lo : lo + step], COPY)
 
         def interleaved(rows, grouped):
             return grouped.rearrange("p (c i) j -> p c j i", i=4), rows.rearrange("p j (c i) -> p c j i", i=4)

@@ -232,24 +232,23 @@ def tile_moe_tk_mlp_relu_kernel(tc, xT, w1, w2, gate, offs, pos1, pos2, pos3, ou
             bank = psum.tile([P, P], F32, name="turned", tag="bank")
             nc.tensor.transpose(bank[:], plain[:], identity[:])
             turned_banks.append(bank)
-        firsts = keep.tile([P, 3 * P], F32, name="firsts", align_bytes=64)
-        nc.scalar.activation(firsts[:, early], picked(0, early), COPY)
+        firsts = keep.tile([P, 2 * P], F32, name="firsts", align_bytes=64)
+        nc.scalar.activation(firsts[:], picked(0, early), COPY)
         back = psum.tile([P, P], F32, name="back", tag="bank")
         for r in range(TOP):
             scaled = keep.tile([P, P], F32, name=f"scaled{r}", align_bytes=64)
             nc.scalar.activation(scaled[:], turned_banks[r][:], COPY, scale=gate_columns[:, r, turned_tile : turned_tile + 1])
             nc.tensor.matmul(back[:], scaled[:], identity[:], start=r == 0, stop=r == TOP - 1, is_transpose=True)
-        nc.scalar.activation(firsts[:, late], picked(0, late), COPY)
         nc.scalar.copy(total[:, turned], back[:])
 
         products = [keep.tile([P, 3 * P], F32, name=f"product{r}", align_bytes=64) for r in range(TOP)]
         pair = keep.tile([P, 3 * P], F32, name="pair", align_bytes=64)
-        for r in (2, 1):
+        for r in (1, 2):
             nc.vector.tensor_tensor(products[r][:], picked(r, direct), gates[:, r, :], MULT)
-        nc.vector.tensor_tensor(products[0][:, early], firsts[:, early], gates[:, 0, early], MULT)
+        nc.vector.tensor_tensor(products[0][:, late], picked(0, late), gates[:, 0, late], MULT)
         nc.vector.tensor_tensor(pair[:], products[1][:], products[2][:], ADD)
-        nc.vector.tensor_tensor(products[0][:, late], firsts[:, late], gates[:, 0, late], MULT)
-        nc.vector.tensor_tensor(total[:, early], pair[:, early], products[0][:, early], ADD)
-        nc.sync.dma_start(out=out[:, : T // 2], in_=total[:, : T // 2])
+        nc.vector.tensor_tensor(products[0][:, early], firsts[:], gates[:, 0, early], MULT)
         nc.vector.tensor_tensor(total[:, late], pair[:, late], products[0][:, late], ADD)
         nc.sync.dma_start(out=out[:, T // 2 :], in_=total[:, T // 2 :])
+        nc.vector.tensor_tensor(total[:, early], pair[:, early], products[0][:, early], ADD)
+        nc.sync.dma_start(out=out[:, : T // 2], in_=total[:, : T // 2])

from contextlib import ExitStack

import concourse.mybir as mybir
from concourse.masks import make_identity

K, T, E, C, H, N, TOP = 2048, 512, 6, 256, 512, 128, 3

FLOPS = 2 * TOP * T * (K * H + H * N)

F32 = mybir.dt.float32
BF16 = mybir.dt.bfloat16
U32 = mybir.dt.uint32
U16 = mybir.dt.uint16
U8 = mybir.dt.uint8
FP8X4 = mybir.dt.float8_e4m3fn_x4
COPY = mybir.ActivationFunctionType.Copy
RELU = mybir.ActivationFunctionType.Relu
ADD = mybir.AluOpType.add
MULT = mybir.AluOpType.mult

P = 128
J = 4
S = K // (P * J)
M = P
HT = H // M
HALF = C // 2
HALVES = ((0, HALF), (HALF, C))
SCALE_ROWS = 4
WINDOW = 2048
DMA_ALIGN = 256
STAGE_BUFS = 11
GROUPED_BUFS = 8
CODE_BUFS = 2 * S
HIDDEN_AT = 1
SCALAR_PIECES = 4
VECTOR_CHUNK = 7
SHARED_FROM = 2
SHARE_CATCHING_UP = 56
CAUGHT_UP = 4
W2_ON_VECTOR = (0, 3, 4)
Y_ON_VECTOR = (3, 4, 6)


def tile_moe_tk_mlp_relu_kernel(tc, xT, w1, w2, gate, offs, pos1, pos2, pos3, out):
    nc = tc.nc
    with ExitStack() as ctx:
        keep = ctx.enter_context(tc.tile_pool(name="keep", bufs=1))
        stage = ctx.enter_context(tc.tile_pool(name="stage", bufs=STAGE_BUFS))
        groups = ctx.enter_context(tc.tile_pool(name="groups", bufs=GROUPED_BUFS))
        codes = ctx.enter_context(tc.tile_pool(name="codes", bufs=CODE_BUFS))
        psum = ctx.enter_context(tc.psum_pool(name="psum", bufs=8))

        def load_pass(rows, pool, tag):
            raw = pool.tile([P, J, rows.shape[1]], F32, name="raw", tag=tag, align_bytes=DMA_ALIGN)
            nc.sync.dma_start(out=raw[:], in_=rows.rearrange("(p j) c -> p j c", j=J))
            return raw[:]

        def shared_copy(dst, src, share):
            if share > 0:
                nc.vector.tensor_copy(out=dst[:, :share], in_=src[:, :share])
            pieces = SCALAR_PIECES if share == 0 else 1
            step = (dst.shape[1] - share) // pieces
            for lo in range(share, dst.shape[1], max(step, 1)):
                nc.scalar.activation(dst[:, lo : lo + step], src[:, lo : lo + step], COPY)

        def interleaved(rows, grouped):
            return grouped.rearrange("p (c i) j -> p c j i", i=4), rows.rearrange("p j (c i) -> p c j i", i=4)

        def quantise(words, scales, values):
            nc.vector.quantize_mx(out=words.bitcast(FP8X4), scales=scales, in_=values)

        def matmul(acc, lhs_words, lhs_scales, rhs_words, rhs_scales, start, stop):
            nc.tensor.matmul_mx(
                out=acc,
                lhsT=lhs_words.bitcast(FP8X4),
                lhsT_scale=lhs_scales,
                rhs=rhs_words.bitcast(FP8X4),
                rhs_scale=rhs_scales,
                start=start,
                stop=stop,
            )

        x_scales = keep.tile([P, WINDOW], U8, name="x_scales", align_bytes=64)
        nc.gpsimd.memset(x_scales[:].bitcast(U32), 0)
        x_words = keep.tile([P, (S - 1) * T + WINDOW], U32, name="x_words", align_bytes=64)
        nc.gpsimd.memset(x_words[:, S * T :], 0)
        identity = keep.tile([P, P], F32, name="identity", align_bytes=64)
        make_identity(nc, identity[:])
        offsets = keep.tile([P, TOP * T // 16], U16, name="offsets")
        for s in range(S):
            if s == S // 2:
                nc.sync.dma_start(offsets[:], offs)
            raw = load_pass(xT[s * P * J : (s + 1) * P * J, :], stage, "raw")
            grouped = groups.tile([P, T, J], BF16, name="x_grouped", tag="grouped", align_bytes=64)
            shared_copy(*interleaved(raw, grouped[:]), T // 4 if s == 0 else 0)
            first = (S - 1 - s) * T
            quantise(x_words[:, first : first + T], x_scales[SCALE_ROWS * s :, :T], grouped[:].rearrange("p t j -> p (t j)"))

        tiles = T // P
        turned_tile = tiles - 1
        gate_rows = keep.tile([P, TOP, P], F32, name="gate_rows", align_bytes=DMA_ALIGN)
        nc.gpsimd.memset(gate_rows[:], 0.0)
        nc.sync.dma_start(out=gate_rows[:tiles], in_=gate[:, 0, :].rearrange("r (i n) -> i r n", n=P))
        turned_rows = psum.tile([P, TOP, P], F32, name="turned_rows", tag="bank")
        for r in range(TOP):
            nc.tensor.transpose(turned_rows[:, r, :], gate_rows[:, r, :], identity[:])
        gate_columns = keep.tile([P, TOP, tiles], F32, name="gate_columns", align_bytes=64)
        nc.scalar.copy(gate_columns[:], turned_rows[:, :, :tiles])
        gates = keep.tile([P, TOP, turned_tile * P], F32, name="gates", align_bytes=64)
        for r in range(TOP):
            spread = psum.tile([P, turned_tile * P], F32, name="spread", tag="bank")
            for i in range(turned_tile):
                column = gate_columns[:, r, i : i + 1].to_broadcast([P, P])
                nc.tensor.transpose(spread[:, i * P : (i + 1) * P], column, identity[:])
            nc.scalar.copy(gates[:, r, :], spread[:])

        def gather(table, dtype, name):
            picked = keep.tile([P, E * C], dtype, name=name, align_bytes=64)
            nc.vector.tensor_copy(picked[:], table.indirect(offsets[:]))
            return picked

        slot_words = [gather(x_words[:, (S - 1 - s) * T :][:, :WINDOW], U32, f"slot_words{s}") for s in range(S)]
        slot_scales = gather(x_scales[:], U8, "slot_scales")

        def quantise_chunk(raw, share, by_tiles):
            grouped = groups.tile([P, H, J], BF16, name="w1_grouped", tag="grouped", align_bytes=64)
            dst = grouped[:].rearrange("p (t m) j -> p m j t", t=HT)
            src = raw.rearrange("p j (m t) -> p m j t", t=HT)
            if by_tiles:
                nc.vector.tensor_copy(out=dst[:, :, :, : HT // 2], in_=src[:, :, :, : HT // 2])
                nc.scalar.activation(dst[:, :, :, HT // 2 :], src[:, :, :, HT // 2 :], COPY)
            else:
                shared_copy(dst, src, share)
            words = codes.tile([P, H], U32, name="w1_words", align_bytes=64)
            scales = codes.tile([P, H], U8, name="w1_scales", align_bytes=64)
            step = M if by_tiles else H
            for lo in range(0, H, step):
                values = grouped[:, lo : lo + step, :].rearrange("p h j -> p (h j)")
                quantise(words[:, lo : lo + step], scales[:, lo : lo + step], values)
            return words, scales

        def relu_out(values, bank):
            nc.scalar.activation(values.rearrange("p (c t) -> p c t", t=HT), bank[:].rearrange("p t c -> p c t"), RELU)

        def quantise_hidden(e, parts):
            words = keep.tile([P, C], U32, name=f"h_words{e}", align_bytes=64)
            scales = keep.tile([P, C], U8, name=f"h_scales{e}", align_bytes=64)
            step = C // len(parts)
            for i, part in enumerate(parts):
                quantise(words[:, i * step : (i + 1) * step], scales[:, i * step : (i + 1) * step], part)
            hidden.append((words, scales))

        hidden = []
        h_banks = []
        for e in range(E):
            banks = [psum.tile([P, HT, HALF], F32, name="h_bank", tag="bank") for half in HALVES]
            for s in range(S):
                raw = load_pass(w1[e, s * P * J : (s + 1) * P * J, :], stage, "raw")
                if e < SHARED_FROM:
                    share = M if e * S + s == VECTOR_CHUNK else 0
                else:
                    share = SHARE_CATCHING_UP if e < CAUGHT_UP else M // 2
                words, scales = quantise_chunk(raw, share, e == E - 1 and s == S - 1)
                for bank, (lo, hi), order in zip(banks, HALVES, (range(HT), reversed(range(HT)))):
                    slots = slice(e * C + lo, e * C + hi)
                    for i, t in enumerate(order):
                        cols = slice(t * M, (t + 1) * M)
                        matmul(
                            bank[:, t, :], words[:, cols], scales[:, cols], slot_words[s][:, slots],
                            slot_scales[SCALE_ROWS * s :, slots], s == 0 and i == 0, s == S - 1 and i == HT - 1,
                        )
                if s == HIDDEN_AT and e > 0:
                    values = raw[:, J - 1, :].bitcast(BF16)
                    for (lo, hi), bank in zip(HALVES, h_banks):
                        relu_out(values[:, lo * HT : hi * HT], bank)
                    quantise_hidden(e - 1, [values])
            h_banks = banks

        w2_raw = [load_pass(w2[e], *((keep, "y") if e == E - 1 else (stage, "raw"))) for e in range(E)]
        y = keep.tile([P, E * C], F32, name="y", tag="y", align_bytes=DMA_ALIGN)

        h_last = [keep.tile([P, HALF * HT], BF16, name=f"h_last{lo}", align_bytes=64) for lo, hi in HALVES]
        for half, bank in zip(h_last, h_banks):
            relu_out(half[:], bank)

        w2_grouped = []
        for e in range(E):
            grouped = keep.tile([P, N, J], BF16, name=f"w2_grouped{e}", align_bytes=64)
            dst, src = interleaved(w2_raw[e], grouped[:])
            if e == E - 1:
                shared_copy(dst, src, dst.shape[1] // 2)
            elif e in W2_ON_VECTOR:
                nc.vector.tensor_copy(out=dst, in_=src)
            else:
                nc.scalar.activation(dst, src, COPY)
            w2_grouped.append(grouped)

        quantise_hidden(E - 1, [half[:] for half in h_last])

        w2_codes = []
        for e in range(E):
            words = keep.tile([P, N], U32, name=f"w2_words{e}", align_bytes=64)
            scales = keep.tile([P, N], U8, name=f"w2_scales{e}", align_bytes=64)
            for lo, hi in ((N // 2, N), (0, N // 2)) if e == E - 1 else ((0, N),):
                quantise(words[:, lo:hi], scales[:, lo:hi], w2_grouped[e][:, lo:hi, :].rearrange("p n j -> p (n j)"))
            w2_codes.append((words, scales))

        pieces = [(e, 0, C) for e in range(E - 1)] + [(E - 1, lo, hi) for lo, hi in HALVES]
        for i, (e, lo, hi) in enumerate(pieces):
            acc = psum.tile([P, C], F32, name="y_bank", tag="bank")
            matmul(
                acc[:, : hi - lo], w2_codes[e][0][:], w2_codes[e][1][:], hidden[e][0][:, lo:hi], hidden[e][1][:, lo:hi],
                True, True,
            )
            copy_out = nc.vector.tensor_copy if i in Y_ON_VECTOR else nc.scalar.copy
            copy_out(y[:, e * C + lo : e * C + hi], acc[:, : hi - lo])

        places = [keep.tile([P, T // 16], U16, name=f"place{r}") for r in range(TOP)]
        for r, pos in enumerate((pos1, pos2, pos3)):
            nc.sync.dma_start(places[r][:], pos)

        def picked(r, cols):
            return y[:].indirect(places[r][:, cols.start // 16 : cols.stop // 16])

        total = keep.tile([P, T], F32, name="total", align_bytes=DMA_ALIGN)
        early, late, direct, turned = slice(0, 2 * P), slice(2 * P, 3 * P), slice(0, 3 * P), slice(3 * P, T)

        turned_banks = []
        for r in range(TOP):
            plain = keep.tile([P, P], F32, name=f"plain{r}", align_bytes=64)
            nc.scalar.activation(plain[:], picked(r, turned), COPY)
            bank = psum.tile([P, P], F32, name="turned", tag="bank")
            nc.tensor.transpose(bank[:], plain[:], identity[:])
            turned_banks.append(bank)
        firsts = keep.tile([P, 2 * P], F32, name="firsts", align_bytes=64)
        nc.scalar.activation(firsts[:], picked(0, early), COPY)
        back = psum.tile([P, P], F32, name="back", tag="bank")
        for r in range(TOP):
            scaled = keep.tile([P, P], F32, name=f"scaled{r}", align_bytes=64)
            nc.scalar.activation(scaled[:], turned_banks[r][:], COPY, scale=gate_columns[:, r, turned_tile : turned_tile + 1])
            nc.tensor.matmul(back[:], scaled[:], identity[:], start=r == 0, stop=r == TOP - 1, is_transpose=True)
        nc.scalar.copy(total[:, turned], back[:])

        products = [keep.tile([P, 3 * P], F32, name=f"product{r}", align_bytes=64) for r in range(TOP)]
        pair = keep.tile([P, 3 * P], F32, name="pair", align_bytes=64)
        for r in (1, 2):
            nc.vector.tensor_tensor(products[r][:], picked(r, direct), gates[:, r, :], MULT)
        nc.vector.tensor_tensor(products[0][:, late], picked(0, late), gates[:, 0, late], MULT)
        nc.vector.tensor_tensor(pair[:], products[1][:], products[2][:], ADD)
        nc.vector.tensor_tensor(products[0][:, early], firsts[:], gates[:, 0, early], MULT)
        nc.vector.tensor_tensor(total[:, late], pair[:, late], products[0][:, late], ADD)
        nc.sync.dma_start(out=out[:, T // 2 :], in_=total[:, T // 2 :])
        nc.vector.tensor_tensor(total[:, early], pair[:, early], products[0][:, early], ADD)
        nc.sync.dma_start(out=out[:, : T // 2], in_=total[:, : T // 2])
